import numpy as np
import ml_dtypes


def mxq(x, axis, fmt="e4m3"):
    dtype, down = {"e4m3": (ml_dtypes.float8_e4m3fn, 7), "e5m2": (ml_dtypes.float8_e5m2, 14)}[fmt]
    v = np.moveaxis(np.asarray(x, np.float32).astype(ml_dtypes.bfloat16).astype(np.float64), axis, -1)
    blocks = v.reshape(v.shape[:-1] + (-1, 32))
    amax = np.abs(blocks).max(-1, keepdims=True)
    byte = np.maximum(np.where(amax > 0, np.frexp(amax)[1] - 1 + 127, 0) - down, 1)
    scale = np.exp2(byte - 127.0)
    codes = (blocks / scale).astype(np.float32).astype(dtype).astype(np.float64)
    return np.moveaxis((codes * scale).reshape(v.shape), -1, axis)


WIDE = False


def mx_kscale(k):
    if not WIDE:
        return np.ones(k)
    levels = np.array([10, -10, 5, -5, 0])
    if k % 512:
        return np.exp2(np.random.permutation(np.resize(levels, k // 32))).repeat(32)
    a = np.empty((k // 512, 16))
    for p in range(k // 512):
        a[p, :8] = np.random.permutation(np.resize(levels, 8))
        for g in range(8):
            far = levels[np.abs(levels - a[p, g]) >= 10]
            a[p, g + 8] = far[np.random.randint(len(far))]
    return np.exp2(a.ravel()).repeat(32)


def f64(x):
    return np.asarray(x).astype(np.float64)


def striped(idx):
    return np.tile(idx.reshape(-1, 16).T, (8, 1)).astype(np.uint16)


def unstriped(offs):
    return offs[:16].T.reshape(-1).astype(np.int64)


def pack_weight(w):
    k, n = w.shape
    w = f64(np.asarray(w, np.float32).astype(ml_dtypes.bfloat16)).reshape(k // 32, 32, n)
    amax = np.abs(w).max(1)
    byte = np.clip(np.where(amax > 0, np.frexp(amax)[1] - 1 + 127 - 7, 1), 1, 254)
    scaled = (w * np.exp2(127.0 - byte)[:, None, :]).reshape(k, n).astype(np.float32)
    words = np.ascontiguousarray(scaled.reshape(k // 512, 128, 4, n).transpose(0, 1, 3, 2)).astype(ml_dtypes.float8_e4m3fn).view(np.uint8)
    return words, np.ascontiguousarray(byte.astype(np.uint8).reshape(k // 512, 16, n))


def unpack_weight(words, scales):
    g, p, n, _ = words.shape
    vals = np.ascontiguousarray(words).view(ml_dtypes.float8_e4m3fn).astype(np.float64) * np.repeat(np.exp2(scales.astype(np.float64) - 127.0), 8, axis=1)[..., None]
    return vals.transpose(0, 1, 3, 2).reshape(g * 512, n)


def relu(v):
    return np.maximum(v, 0.0)


K, T, S, V, N, U = 512, 1024, 512, 256, 256, 512


def setup_inputs():
    n = np.random.standard_normal
    s = mx_kscale(K)[:, None]
    packed_w1 = pack_weight(n((K, N)) / np.sqrt(2 * K) / s)
    packed_w2 = pack_weight(n((K, N)) / np.sqrt(2 * K) / s)
    return {
        "xT": (n((K, T)) * s).astype(np.float32),
        "w1_words": packed_w1[0],
        "w1_scales": packed_w1[1],
        "w2_words": packed_w2[0],
        "w2_scales": packed_w2[1],
        "offs": striped(np.random.permutation(T)[:S]),
        "to1": striped(np.random.permutation(U)[:V]),
        "to2": striped(np.random.permutation(U)[:V]),
    }


def reference(xT, w1_words, w1_scales, w2_words, w2_scales, offs, to1, to2):
    xq = mxq(f64(xT)[:, unstriped(offs)], 0, "e4m3")
    o0 = np.zeros((N, S))
    o0[:, unstriped(to1)] = unpack_weight(w1_words, w1_scales).T @ xq[:, :V]
    o1 = np.zeros((N, S))
    o1[:, unstriped(to2)] = unpack_weight(w2_words, w2_scales).T @ xq[:, V:2 * V]
    return relu(o0 + o1)

@@ -1,0 +1,169 @@
+from contextlib import ExitStack
+
+import concourse.mybir as mybir
+from concourse.masks import make_identity
+
+K, T, S, V, N, U = 512, 1024, 512, 256, 256, 512
+FLOPS = 2 * K * N * S
+
+F32 = mybir.dt.float32
+BF16 = mybir.dt.bfloat16
+I32 = mybir.dt.int32
+U32 = mybir.dt.uint32
+U16 = mybir.dt.uint16
+U8 = mybir.dt.uint8
+FP8X4 = mybir.dt.float8_e4m3fn_x4
+RELU = mybir.ActivationFunctionType.Relu
+ADD = mybir.AluOpType.add
+
+P = 128
+PACK = 4
+GROUP = 16
+PIECE = 128
+HALF = U // 2
+
+
+def tile_picked_spconv_relu_e_kernel(
+    tc, xT, w1_words, w1_scales, w2_words, w2_scales, offs, to1, to2, out
+):
+    nc = tc.nc
+    with ExitStack() as ctx:
+        keep = ctx.enter_context(tc.tile_pool(name="keep", bufs=1))
+        psum = ctx.enter_context(tc.psum_pool(name="psum", bufs=1))
+
+        picks = keep.tile([P, S // GROUP], U16, name="picks")
+        places = [keep.tile([P, V // GROUP], U16, name=f"places{d}") for d in range(2)]
+        rows = [keep.tile([P, T], F32, name=f"rows{j}") for j in range(PACK)]
+        w_codes = [keep.tile([P, N], U32, name=f"w_codes{d}", align_bytes=64) for d in range(2)]
+        w_scales = [keep.tile([P, N], U8, name=f"w_scales{d}", align_bytes=64) for d in range(2)]
+        spread = [[keep.tile([P, U], F32, name=f"spread{d}{b}") for b in range(2)] for d in range(2)]
+        ident = keep.tile([P, P], F32, name="ident")
+        zero = keep.tile([P, 1], F32, name="zero")
+        zero_bias = keep.tile([P, 1], F32, name="zero_bias")
+
+        for d in range(2):
+            nc.gpsimd.memset(w_scales[d][:].bitcast(I32), 0)
+        nc.vector.memset(zero[:], 0.0)
+        nc.scalar.activation(zero_bias[:], zero[:], RELU)
+
+        x_rows = xT.rearrange("(p j) t -> j p t", j=PACK)
+
+        def load_words(d, words):
+            nc.sync.dma_start(w_codes[d][:].bitcast(I32), words[0].rearrange("p n r -> p (n r)").bitcast(I32))
+
+        def load_scales(engine, d, scales):
+            for q in range(4):
+                engine.dma_start(
+                    w_scales[d][32 * q : 32 * q + 4, :].bitcast(I32), scales[0, 4 * q : 4 * q + 4, :].bitcast(I32)
+                )
+
+        nc.sync.dma_start(rows[0][:], x_rows[0])
+        nc.sync.dma_start(picks[:], offs)
+        for j in range(1, PACK):
+            nc.sync.dma_start(rows[j][:], x_rows[j])
+        load_words(0, w1_words)
+        load_scales(nc.sync, 0, w1_scales)
+        load_words(1, w2_words)
+        nc.sync.dma_start(places[0][:], to1)
+        nc.sync.dma_start(places[1][:], to2)
+        load_scales(nc.gpsimd, 1, w2_scales)
+        make_identity(nc, ident[:])
+
+        for d in range(2):
+            for b in range(2):
+                nc.vector.memset(spread[d][b][:], 0.0)
+
+        turns = [(0, 0), (1, 0), (0, 1), (1, 1)]
+        picked = keep.tile([P, PACK, S], F32, name="picked")
+        for j in range(PACK - 1):
+            nc.vector.tensor_copy(picked[:, j, :], rows[j][:].indirect(picks[:]))
+
+        x_codes = [keep.tile([P, V], U32, name=f"x_codes{d}", align_bytes=64) for d in range(2)]
+        x_scales = [keep.tile([P, V], U8, name=f"x_scales{d}", align_bytes=64) for d in range(2)]
+        woven = {t: keep.tile([P, PIECE * PACK], BF16, name=f"woven{t[0]}{t[1]}", align_bytes=64) for t in turns}
+
+        def gather_last(d, h):
+            e0 = d * V + h * PIECE
+            nc.vector.tensor_copy(
+                picked[:, PACK - 1, e0 : e0 + PIECE],
+                rows[PACK - 1][:].indirect(picks[:, e0 // GROUP : (e0 + PIECE) // GROUP]),
+            )
+
+        def weave(d, h):
+            e0 = d * V + h * PIECE
+            nc.scalar.copy(
+                woven[(d, h)][:].rearrange("p (c i j) -> p c j i", i=4, j=PACK),
+                picked[:, :, e0 : e0 + PIECE].rearrange("p j (c i) -> p c j i", i=4),
+            )
+
+        def quantise(d, h):
+            cols = slice(h * PIECE, (h + 1) * PIECE)
+            nc.vector.quantize_mx(out=x_codes[d][:, cols].bitcast(FP8X4), scales=x_scales[d][:, cols], in_=woven[(d, h)][:])
+
+        def product(d, b, cols, name, acc):
+            width = cols.stop - cols.start
+            m_cols = slice(b * P, (b + 1) * P)
+            nc.tensor.matmul_mx(
+                out=acc,
+                lhsT=w_codes[d][:, m_cols].bitcast(FP8X4),
+                lhsT_scale=w_scales[d][:, m_cols],
+                rhs=x_codes[d][:, cols].bitcast(FP8X4),
+                rhs_scale=x_scales[d][:, cols],
+                start=True,
+                stop=True,
+            )
+            y = keep.tile([P, width], F32, name=f"y{name}")
+            nc.scalar.copy(y[:], acc)
+            return y
+
+        def scatter(d, b, cols, y):
+            nc.vector.tensor_copy(
+                spread[d][b][:].indirect(places[d][:, cols.start // GROUP : cols.stop // GROUP]), y[:]
+            )
+
+        banks = [psum.tile([P, U], F32, name=f"bank{i}") for i in range(7)]
+        for d, h in turns:
+            gather_last(d, h)
+        weave(*turns[0])
+        for i, (d, h) in enumerate(turns):
+            if i + 1 < len(turns):
+                weave(*turns[i + 1])
+            quantise(d, h)
+            cols = slice(h * PIECE, (h + 1) * PIECE)
+            y = product(d, 0, cols, f"{d}0{h}", banks[i][:, 0:PIECE])
+            scatter(d, 0, cols, y)
+        ys = [product(d, 1, slice(0, V), f"{d}1", banks[3 + d][:, V : 2 * V]) for d in range(2)]
+        for d in range(2):
+            scatter(d, 1, slice(0, V), ys[d])
+
+        turned = [keep.tile([P, HALF], F32, name=f"turned{h}") for h in range(2)]
+        result0 = keep.tile([P, U], F32, name="result0")
+        for h in range(2):
+            for c in range(HALF // P):
+                cols = slice(h * HALF + c * P, h * HALF + (c + 1) * P)
+                for d in range(2):
+                    nc.tensor.matmul(
+                        banks[5 + h][:, c * P : (c + 1) * P],
+                        spread[d][0][:, cols],
+                        ident[:],
+                        start=(d == 0),
+                        stop=(d == 1),
+                        is_transpose=True,
+                    )
+            nc.scalar.activation(turned[h][:], banks[5 + h][:, 0:HALF], RELU, bias=zero_bias[:])
+        for h in range(2):
+            for c in range(HALF // P):
+                cols = slice(c * P, (c + 1) * P)
+                nc.tensor.transpose(banks[h][:, cols], turned[h][:, cols], ident[:])
+            nc.scalar.copy(result0[:, h * HALF : (h + 1) * HALF], banks[h][:, 0:HALF])
+        nc.scalar.dma_start(out[0:P, :], result0[:])
+
+        total = [keep.tile([P, HALF], F32, name=f"total{h}") for h in range(2)]
+        result1 = keep.tile([P, HALF], F32, name="result1")
+        for h in range(2):
+            cols = slice(h * HALF, (h + 1) * HALF)
+            nc.vector.tensor_tensor(total[h][:], spread[0][1][:, cols], spread[1][1][:, cols], ADD)
+        nc.scalar.activation(turned[1][:], total[0][:], RELU, bias=zero_bias[:])
+        nc.scalar.dma_start(out[P : 2 * P, 0:HALF], turned[1][:])
+        nc.vector.tensor_scalar_max(result1[:], total[1][:], 0.0)
+        nc.sync.dma_start(out[P : 2 * P, HALF:U], result1[:])

@@ -13,6 +13,7 @@ U32 = mybir.dt.uint32
 U16 = mybir.dt.uint16
 U8 = mybir.dt.uint8
 FP8X4 = mybir.dt.float8_e4m3fn_x4
+COPY = mybir.ActivationFunctionType.Copy
 RELU = mybir.ActivationFunctionType.Relu
 ADD = mybir.AluOpType.add
 
@@ -51,90 +52,98 @@ def tile_picked_spconv_relu_e_kernel(
         def load_words(d, words):
             nc.sync.dma_start(w_codes[d][:].bitcast(I32), words[0].rearrange("p n r -> p (n r)").bitcast(I32))
 
-        def load_scales(engine, d, scales):
-            for q in range(4):
+        def load_scales(engine, d, scales, quadrants):
+            for q in quadrants:
                 engine.dma_start(
                     w_scales[d][32 * q : 32 * q + 4, :].bitcast(I32), scales[0, 4 * q : 4 * q + 4, :].bitcast(I32)
                 )
 
         nc.sync.dma_start(rows[0][:], x_rows[0])
         nc.sync.dma_start(picks[:], offs)
-        for j in range(1, PACK):
-            nc.sync.dma_start(rows[j][:], x_rows[j])
-        load_words(0, w1_words)
-        load_scales(nc.sync, 0, w1_scales)
-        load_words(1, w2_words)
+        nc.sync.dma_start(rows[1][:], x_rows[1])
         nc.sync.dma_start(places[0][:], to1)
+        nc.sync.dma_start(rows[2][:], x_rows[2])
         nc.sync.dma_start(places[1][:], to2)
-        load_scales(nc.gpsimd, 1, w2_scales)
+        nc.sync.dma_start(rows[3][:], x_rows[3])
+        load_words(0, w1_words)
+        load_scales(nc.sync, 0, w1_scales, range(4))
+        load_words(1, w2_words)
+        load_scales(nc.sync, 1, w2_scales, range(1))
+        load_scales(nc.gpsimd, 1, w2_scales, range(1, 4))
         make_identity(nc, ident[:])
 
         for d in range(2):
             for b in range(2):
                 nc.vector.memset(spread[d][b][:], 0.0)
 
-        turns = [(0, 0), (1, 0), (0, 1), (1, 1)]
-        picked = keep.tile([P, PACK, S], F32, name="picked")
-        for j in range(PACK - 1):
-            nc.vector.tensor_copy(picked[:, j, :], rows[j][:].indirect(picks[:]))
+        pieces = [(0, 0, PIECE), (1, 0, PIECE), (0, PIECE, V), (1, PIECE, V)]
+        LATER = PACK - 1
+        picked = keep.tile([P, LATER, S], F32, name="picked")
+        woven_all = keep.tile([P, S * PACK], BF16, name="woven_all", align_bytes=64)
+        woven = [woven_all[:, (d * V + c0) * PACK : (d * V + c1) * PACK] for d, c0, c1 in pieces]
+
+        def picks_of(i):
+            d, c0, c1 = pieces[i]
+            return picks[:, (d * V + c0) // GROUP : (d * V + c1) // GROUP]
+
+        row0 = keep.tile([P, T], BF16, name="row0")
+        nc.scalar.copy(row0[:], rows[0][:])
+        nc.scalar.activation(
+            woven_all[:].rearrange("p (c j) -> p c j", j=PACK)[:, :, 0], row0[:].indirect(picks[:]), COPY
+        )
+        for j in range(1, PACK - 1):
+            nc.vector.tensor_copy(picked[:, j - 1, :], rows[j][:].indirect(picks[:]))
 
         x_codes = [keep.tile([P, V], U32, name=f"x_codes{d}", align_bytes=64) for d in range(2)]
         x_scales = [keep.tile([P, V], U8, name=f"x_scales{d}", align_bytes=64) for d in range(2)]
-        woven = {t: keep.tile([P, PIECE * PACK], BF16, name=f"woven{t[0]}{t[1]}", align_bytes=64) for t in turns}
 
-        def gather_last(d, h):
-            e0 = d * V + h * PIECE
-            nc.vector.tensor_copy(
-                picked[:, PACK - 1, e0 : e0 + PIECE],
-                rows[PACK - 1][:].indirect(picks[:, e0 // GROUP : (e0 + PIECE) // GROUP]),
-            )
+        def gather_last(i):
+            d, c0, c1 = pieces[i]
+            nc.vector.tensor_copy(picked[:, LATER - 1, d * V + c0 : d * V + c1], rows[PACK - 1][:].indirect(picks_of(i)))
 
-        def weave(d, h):
-            e0 = d * V + h * PIECE
+        def weave(i):
+            d, c0, c1 = pieces[i]
             nc.scalar.copy(
-                woven[(d, h)][:].rearrange("p (c i j) -> p c j i", i=4, j=PACK),
-                picked[:, :, e0 : e0 + PIECE].rearrange("p j (c i) -> p c j i", i=4),
+                woven[i].rearrange("p (c i j) -> p c j i", i=4, j=PACK)[:, :, 1:PACK, :],
+                picked[:, :, d * V + c0 : d * V + c1].rearrange("p j (c i) -> p c j i", i=4),
             )
 
-        def quantise(d, h):
-            cols = slice(h * PIECE, (h + 1) * PIECE)
-            nc.vector.quantize_mx(out=x_codes[d][:, cols].bitcast(FP8X4), scales=x_scales[d][:, cols], in_=woven[(d, h)][:])
+        def quantise(i):
+            d, c0, c1 = pieces[i]
+            nc.vector.quantize_mx(out=x_codes[d][:, c0:c1].bitcast(FP8X4), scales=x_scales[d][:, c0:c1], in_=woven[i])
 
-        def product(d, b, cols, name, acc):
-            width = cols.stop - cols.start
+        def product(d, b, c0, c1, acc):
             m_cols = slice(b * P, (b + 1) * P)
             nc.tensor.matmul_mx(
                 out=acc,
                 lhsT=w_codes[d][:, m_cols].bitcast(FP8X4),
                 lhsT_scale=w_scales[d][:, m_cols],
-                rhs=x_codes[d][:, cols].bitcast(FP8X4),
-                rhs_scale=x_scales[d][:, cols],
+                rhs=x_codes[d][:, c0:c1].bitcast(FP8X4),
+                rhs_scale=x_scales[d][:, c0:c1],
                 start=True,
                 stop=True,
             )
-            y = keep.tile([P, width], F32, name=f"y{name}")
+            y = keep.tile([P, c1 - c0], F32, name=f"y{d}{b}{c0}")
             nc.scalar.copy(y[:], acc)
             return y
 
-        def scatter(d, b, cols, y):
-            nc.vector.tensor_copy(
-                spread[d][b][:].indirect(places[d][:, cols.start // GROUP : cols.stop // GROUP]), y[:]
-            )
+        def scatter(d, b, c0, c1, y):
+            nc.vector.tensor_copy(spread[d][b][:].indirect(places[d][:, c0 // GROUP : c1 // GROUP]), y[:])
 
         banks = [psum.tile([P, U], F32, name=f"bank{i}") for i in range(7)]
-        for d, h in turns:
-            gather_last(d, h)
-        weave(*turns[0])
-        for i, (d, h) in enumerate(turns):
-            if i + 1 < len(turns):
-                weave(*turns[i + 1])
-            quantise(d, h)
-            cols = slice(h * PIECE, (h + 1) * PIECE)
-            y = product(d, 0, cols, f"{d}0{h}", banks[i][:, 0:PIECE])
-            scatter(d, 0, cols, y)
-        ys = [product(d, 1, slice(0, V), f"{d}1", banks[3 + d][:, V : 2 * V]) for d in range(2)]
+        for i in range(4):
+            gather_last(i)
+        weave(0)
+        ys0 = []
+        for i, (d, c0, c1) in enumerate(pieces):
+            if i + 1 < len(pieces):
+                weave(i + 1)
+            quantise(i)
+            ys0.append(product(d, 0, c0, c1, banks[i][:, 0 : c1 - c0]))
+            scatter(d, 0, c0, c1, ys0[i])
+        ys = [product(d, 1, 0, V, banks[3 + d][:, V : 2 * V]) for d in range(2)]
         for d in range(2):
-            scatter(d, 1, slice(0, V), ys[d])
+            scatter(d, 1, 0, V, ys[d])
 
         turned = [keep.tile([P, HALF], F32, name=f"turned{h}") for h in range(2)]
         result0 = keep.tile([P, U], F32, name="result0")
@@ -157,13 +166,14 @@ def tile_picked_spconv_relu_e_kernel(
                 nc.tensor.transpose(banks[h][:, cols], turned[h][:, cols], ident[:])
             nc.scalar.copy(result0[:, h * HALF : (h + 1) * HALF], banks[h][:, 0:HALF])
         nc.scalar.dma_start(out[0:P, :], result0[:])
+        late = turned[1][:]
 
         total = [keep.tile([P, HALF], F32, name=f"total{h}") for h in range(2)]
         result1 = keep.tile([P, HALF], F32, name="result1")
         for h in range(2):
             cols = slice(h * HALF, (h + 1) * HALF)
             nc.vector.tensor_tensor(total[h][:], spread[0][1][:, cols], spread[1][1][:, cols], ADD)
-        nc.scalar.activation(turned[1][:], total[0][:], RELU, bias=zero_bias[:])
-        nc.scalar.dma_start(out[P : 2 * P, 0:HALF], turned[1][:])
+        nc.scalar.activation(late, total[0][:], RELU, bias=zero_bias[:])
+        nc.scalar.dma_start(out[P : 2 * P, 0:HALF], late)
         nc.vector.tensor_scalar_max(result1[:], total[1][:], 0.0)
         nc.sync.dma_start(out[P : 2 * P, HALF:U], result1[:])

@@ -1,7 +1,6 @@
 from contextlib import ExitStack
 
 import concourse.mybir as mybir
-from concourse.masks import make_identity
 
 K, T, S, V, N, U = 512, 1024, 512, 256, 256, 512
 FLOPS = 2 * K * N * S
@@ -38,7 +37,7 @@ def tile_picked_spconv_relu_e_kernel(
         w_codes = [keep.tile([P, N], U32, name=f"w_codes{d}", align_bytes=64) for d in range(2)]
         w_scales = [keep.tile([P, N], U8, name=f"w_scales{d}", align_bytes=64) for d in range(2)]
         spread = [[keep.tile([P, U], F32, name=f"spread{d}{b}") for b in range(2)] for d in range(2)]
-        ident = keep.tile([P, P], F32, name="ident")
+
         zero = keep.tile([P, 1], F32, name="zero")
         zero_bias = keep.tile([P, 1], F32, name="zero_bias")
 
@@ -68,15 +67,15 @@ def tile_picked_spconv_relu_e_kernel(
         load_words(0, w1_words)
         load_scales(nc.sync, 0, w1_scales, range(4))
         load_words(1, w2_words)
-        load_scales(nc.sync, 1, w2_scales, range(1))
-        load_scales(nc.gpsimd, 1, w2_scales, range(1, 4))
-        make_identity(nc, ident[:])
+        load_scales(nc.sync, 1, w2_scales, range(2))
+        load_scales(nc.gpsimd, 1, w2_scales, range(2, 4))
+
 
         for d in range(2):
             for b in range(2):
                 nc.vector.memset(spread[d][b][:], 0.0)
 
-        pieces = [(0, 0, PIECE), (1, 0, PIECE), (0, PIECE, V), (1, PIECE, V)]
+        pieces = [(0, 0, PIECE), (0, PIECE, V), (1, 0, V)]
         LATER = PACK - 1
         picked = keep.tile([P, LATER, S], F32, name="picked")
         woven_all = keep.tile([P, S * PACK], BF16, name="woven_all", align_bytes=64)
@@ -130,43 +129,25 @@ def tile_picked_spconv_relu_e_kernel(
         def scatter(d, b, c0, c1, y):
             nc.vector.tensor_copy(spread[d][b][:].indirect(places[d][:, c0 // GROUP : c1 // GROUP]), y[:])
 
-        banks = [psum.tile([P, U], F32, name=f"bank{i}") for i in range(7)]
-        for i in range(4):
+        banks = [psum.tile([P, U], F32, name=f"bank{i}") for i in range(6)]
+        for i in range(len(pieces)):
             gather_last(i)
         weave(0)
-        ys0 = []
         for i, (d, c0, c1) in enumerate(pieces):
             if i + 1 < len(pieces):
                 weave(i + 1)
             quantise(i)
-            ys0.append(product(d, 0, c0, c1, banks[i][:, 0 : c1 - c0]))
-            scatter(d, 0, c0, c1, ys0[i])
-        ys = [product(d, 1, 0, V, banks[3 + d][:, V : 2 * V]) for d in range(2)]
-        for d in range(2):
-            scatter(d, 1, 0, V, ys[d])
+            for b in range(2):
+                scatter(d, b, c0, c1, product(d, b, c0, c1, banks[2 * i + b][:, 0 : c1 - c0]))
 
-        turned = [keep.tile([P, HALF], F32, name=f"turned{h}") for h in range(2)]
-        result0 = keep.tile([P, U], F32, name="result0")
+        sum0 = [keep.tile([P, HALF], F32, name=f"sum0{h}") for h in range(2)]
+        result0 = [keep.tile([P, HALF], F32, name=f"result0{h}") for h in range(2)]
         for h in range(2):
-            for c in range(HALF // P):
-                cols = slice(h * HALF + c * P, h * HALF + (c + 1) * P)
-                for d in range(2):
-                    nc.tensor.matmul(
-                        banks[5 + h][:, c * P : (c + 1) * P],
-                        spread[d][0][:, cols],
-                        ident[:],
-                        start=(d == 0),
-                        stop=(d == 1),
-                        is_transpose=True,
-                    )
-            nc.scalar.activation(turned[h][:], banks[5 + h][:, 0:HALF], RELU, bias=zero_bias[:])
-        for h in range(2):
-            for c in range(HALF // P):
-                cols = slice(c * P, (c + 1) * P)
-                nc.tensor.transpose(banks[h][:, cols], turned[h][:, cols], ident[:])
-            nc.scalar.copy(result0[:, h * HALF : (h + 1) * HALF], banks[h][:, 0:HALF])
-        nc.scalar.dma_start(out[0:P, :], result0[:])
-        late = turned[1][:]
+            cols = slice(h * HALF, (h + 1) * HALF)
+            nc.gpsimd.tensor_tensor(sum0[h][:], spread[0][0][:, cols], spread[1][0][:, cols], ADD)
+            nc.scalar.activation(result0[h][:], sum0[h][:], RELU, bias=zero_bias[:])
+            nc.scalar.dma_start(out[0:P, cols], result0[h][:])
+        late = sum0[1][:]
 
         total = [keep.tile([P, HALF], F32, name=f"total{h}") for h in range(2)]
         result1 = keep.tile([P, HALF], F32, name="result1")

@@ -59,16 +59,14 @@ def tile_picked_spconv_relu_e_kernel(
 
         nc.sync.dma_start(rows[0][:], x_rows[0])
         nc.sync.dma_start(picks[:], offs)
-        nc.sync.dma_start(rows[1][:], x_rows[1])
-        nc.sync.dma_start(places[0][:], to1)
-        nc.sync.dma_start(rows[2][:], x_rows[2])
-        nc.sync.dma_start(places[1][:], to2)
-        nc.sync.dma_start(rows[3][:], x_rows[3])
+        for j in range(1, PACK):
+            nc.sync.dma_start(rows[j][:], x_rows[j])
         load_words(0, w1_words)
         load_scales(nc.sync, 0, w1_scales, range(4))
+        nc.sync.dma_start(places[0][:], to1)
         load_words(1, w2_words)
-        load_scales(nc.sync, 1, w2_scales, range(2))
-        load_scales(nc.gpsimd, 1, w2_scales, range(2, 4))
+        load_scales(nc.sync, 1, w2_scales, range(4))
+        nc.sync.dma_start(places[1][:], to2)
 
 
         for d in range(2):

@@ -79,10 +79,6 @@ def tile_picked_spconv_relu_e_kernel(
         woven_all = keep.tile([P, S * PACK], BF16, name="woven_all", align_bytes=64)
         woven = [woven_all[:, (d * V + c0) * PACK : (d * V + c1) * PACK] for d, c0, c1 in pieces]
 
-        def picks_of(i):
-            d, c0, c1 = pieces[i]
-            return picks[:, (d * V + c0) // GROUP : (d * V + c1) // GROUP]
-
         row0 = keep.tile([P, T], BF16, name="row0")
         nc.scalar.copy(row0[:], rows[0][:])
         nc.scalar.activation(
@@ -94,15 +90,15 @@ def tile_picked_spconv_relu_e_kernel(
         x_codes = [keep.tile([P, V], U32, name=f"x_codes{d}", align_bytes=64) for d in range(2)]
         x_scales = [keep.tile([P, V], U8, name=f"x_scales{d}", align_bytes=64) for d in range(2)]
 
-        def gather_last(i):
-            d, c0, c1 = pieces[i]
-            nc.vector.tensor_copy(picked[:, LATER - 1, d * V + c0 : d * V + c1], rows[PACK - 1][:].indirect(picks_of(i)))
+        def gather_last(e0):
+            offsets = picks[:, e0 // GROUP : (e0 + PIECE) // GROUP]
+            nc.vector.tensor_copy(picked[:, LATER - 1, e0 : e0 + PIECE], rows[PACK - 1][:].indirect(offsets))
 
-        def weave(i):
-            d, c0, c1 = pieces[i]
+        def weave(e0):
+            target = woven_all[:, e0 * PACK : (e0 + PIECE) * PACK]
             nc.scalar.copy(
-                woven[i].rearrange("p (c i j) -> p c j i", i=4, j=PACK)[:, :, 1:PACK, :],
-                picked[:, :, d * V + c0 : d * V + c1].rearrange("p j (c i) -> p c j i", i=4),
+                target.rearrange("p (c i j) -> p c j i", i=4, j=PACK)[:, :, 1:PACK, :],
+                picked[:, :, e0 : e0 + PIECE].rearrange("p j (c i) -> p c j i", i=4),
             )
 
         def quantise(i):
@@ -128,12 +124,11 @@ def tile_picked_spconv_relu_e_kernel(
             nc.vector.tensor_copy(spread[d][b][:].indirect(places[d][:, c0 // GROUP : c1 // GROUP]), y[:])
 
         banks = [psum.tile([P, U], F32, name=f"bank{i}") for i in range(6)]
-        for i in range(len(pieces)):
-            gather_last(i)
-        weave(0)
+        for e0 in range(0, S, PIECE):
+            gather_last(e0)
+        for e0 in range(0, S, PIECE):
+            weave(e0)
         for i, (d, c0, c1) in enumerate(pieces):
-            if i + 1 < len(pieces):
-                weave(i + 1)
             quantise(i)
             for b in range(2):
                 scatter(d, b, c0, c1, product(d, b, c0, c1, banks[2 * i + b][:, 0 : c1 - c0]))

@@ -15,11 +15,11 @@ FP8X4 = mybir.dt.float8_e4m3fn_x4
 COPY = mybir.ActivationFunctionType.Copy
 RELU = mybir.ActivationFunctionType.Relu
 ADD = mybir.AluOpType.add
+MULT = mybir.AluOpType.mult
 
 P = 128
 PACK = 4
 GROUP = 16
-PIECE = 128
 HALF = U // 2
 
 
@@ -57,53 +57,36 @@ def tile_picked_spconv_relu_e_kernel(
                     w_scales[d][32 * q : 32 * q + 4, :].bitcast(I32), scales[0, 4 * q : 4 * q + 4, :].bitcast(I32)
                 )
 
+        load_scales(nc.scalar, 0, w1_scales, range(4))
         nc.sync.dma_start(rows[0][:], x_rows[0])
         nc.sync.dma_start(picks[:], offs)
         for j in range(1, PACK):
             nc.sync.dma_start(rows[j][:], x_rows[j])
         load_words(0, w1_words)
-        load_scales(nc.sync, 0, w1_scales, range(4))
         nc.sync.dma_start(places[0][:], to1)
         load_words(1, w2_words)
         load_scales(nc.sync, 1, w2_scales, range(4))
         nc.sync.dma_start(places[1][:], to2)
 
-
         for d in range(2):
             for b in range(2):
                 nc.vector.memset(spread[d][b][:], 0.0)
 
-        pieces = [(0, 0, PIECE), (0, PIECE, V), (1, 0, V)]
-        LATER = PACK - 1
-        picked = keep.tile([P, LATER, S], F32, name="picked")
-        woven_all = keep.tile([P, S * PACK], BF16, name="woven_all", align_bytes=64)
-        woven = [woven_all[:, (d * V + c0) * PACK : (d * V + c1) * PACK] for d, c0, c1 in pieces]
-
-        row0 = keep.tile([P, T], BF16, name="row0")
-        nc.scalar.copy(row0[:], rows[0][:])
-        nc.scalar.activation(
-            woven_all[:].rearrange("p (c j) -> p c j", j=PACK)[:, :, 0], row0[:].indirect(picks[:]), COPY
-        )
-        for j in range(1, PACK - 1):
-            nc.vector.tensor_copy(picked[:, j - 1, :], rows[j][:].indirect(picks[:]))
-
         x_codes = [keep.tile([P, V], U32, name=f"x_codes{d}", align_bytes=64) for d in range(2)]
         x_scales = [keep.tile([P, V], U8, name=f"x_scales{d}", align_bytes=64) for d in range(2)]
 
-        def gather_last(e0):
-            offsets = picks[:, e0 // GROUP : (e0 + PIECE) // GROUP]
-            nc.vector.tensor_copy(picked[:, LATER - 1, e0 : e0 + PIECE], rows[PACK - 1][:].indirect(offsets))
+        def offsets(d, c0, c1):
+            return picks[:, (d * V + c0) // GROUP : (d * V + c1) // GROUP]
 
-        def weave(e0):
-            target = woven_all[:, e0 * PACK : (e0 + PIECE) * PACK]
-            nc.scalar.copy(
-                target.rearrange("p (c i j) -> p c j i", i=4, j=PACK)[:, :, 1:PACK, :],
-                picked[:, :, e0 : e0 + PIECE].rearrange("p j (c i) -> p c j i", i=4),
+        def plane(woven, j, c0, c1):
+            return woven[:].rearrange("p (c j) -> p c j", j=PACK)[:, c0:c1, j]
+
+        def quantise(d, woven, c0, c1):
+            nc.vector.quantize_mx(
+                out=x_codes[d][:, c0:c1].bitcast(FP8X4),
+                scales=x_scales[d][:, c0:c1],
+                in_=woven,
             )
-
-        def quantise(i):
-            d, c0, c1 = pieces[i]
-            nc.vector.quantize_mx(out=x_codes[d][:, c0:c1].bitcast(FP8X4), scales=x_scales[d][:, c0:c1], in_=woven[i])
 
         def product(d, b, c0, c1, acc):
             m_cols = slice(b * P, (b + 1) * P)
@@ -116,22 +99,60 @@ def tile_picked_spconv_relu_e_kernel(
                 start=True,
                 stop=True,
             )
-            y = keep.tile([P, c1 - c0], F32, name=f"y{d}{b}{c0}")
-            nc.scalar.copy(y[:], acc)
-            return y
 
         def scatter(d, b, c0, c1, y):
-            nc.vector.tensor_copy(spread[d][b][:].indirect(places[d][:, c0 // GROUP : c1 // GROUP]), y[:])
+            nc.vector.tensor_copy(spread[d][b][:].indirect(places[d][:, c0 // GROUP : c1 // GROUP]), y)
 
         banks = [psum.tile([P, U], F32, name=f"bank{i}") for i in range(6)]
-        for e0 in range(0, S, PIECE):
-            gather_last(e0)
-        for e0 in range(0, S, PIECE):
-            weave(e0)
-        for i, (d, c0, c1) in enumerate(pieces):
-            quantise(i)
+
+        PIECE = V // 2
+        cuts = [(0, PIECE), (PIECE, V)]
+        woven_a = keep.tile([P, PIECE * PACK], BF16, name="woven_a", tag="turns", align_bytes=64)
+        woven_b = keep.tile([P, PIECE * PACK], BF16, name="woven_b", align_bytes=64)
+        woven0 = [woven_a, woven_b]
+        woven1 = keep.tile([P, V * PACK], BF16, name="woven1", align_bytes=64)
+
+        def gather0(i, j):
+            c0, c1 = cuts[i]
+            nc.vector.tensor_copy(plane(woven0[i], j, 0, PIECE), rows[j][:].indirect(offsets(0, c0, c1)))
+
+        rounded = [keep.tile([P, T], BF16, name=f"rounded{j}") for j in range(PACK - 1)]
+
+        for j in range(PACK - 1):
+            for i in range(2):
+                gather0(i, j)
+            if j == 0:
+                nc.scalar.copy(rounded[j][:], rows[j][:])
+            else:
+                nc.gpsimd.tensor_copy(rounded[j][:], rows[j][:])
+            nc.scalar.activation(plane(woven1, j, 0, V), rounded[j][:].indirect(offsets(1, 0, V)), COPY)
+
+        LAST = PACK - 1
+        for i in range(2):
+            gather0(i, LAST)
+        for i, (c0, c1) in enumerate(cuts):
+            quantise(0, woven0[i][:], c0, c1)
             for b in range(2):
-                scatter(d, b, c0, c1, product(d, b, c0, c1, banks[2 * i + b][:, 0 : c1 - c0]))
+                product(0, b, c0, c1, banks[2 * i + b][:, 0:PIECE])
+        picked = keep.tile([P, V], F32, name="picked", tag="turns", align_bytes=64)
+        nc.vector.tensor_copy(picked[:], rows[LAST][:].indirect(offsets(1, 0, V)))
+
+        def put(i, b, y):
+            c0, c1 = cuts[i]
+            nc.scalar.copy(y[:], banks[2 * i + b][:, 0:PIECE])
+            scatter(0, b, c0, c1, y[:])
+
+        for b in range(2):
+            put(0, b, keep.tile([P, PIECE], F32, name=f"y0{b}"))
+        nc.scalar.copy(plane(woven1, LAST, 0, V), picked[:])
+        quantise(1, woven1[:], 0, V)
+        put(1, 0, keep.tile([P, PIECE], F32, name="y10", tag="turns", align_bytes=64))
+        put(1, 1, keep.tile([P, PIECE], F32, name="y11"))
+        for b in range(2):
+            product(1, b, 0, V, banks[4 + b][:, 0:V])
+            y = keep.tile([P, V], F32, name=f"y_tap1{b}")
+            nc.scalar.copy(y[:], banks[4 + b][:, 0:V])
+            scatter(1, b, 0, V, y[:])
 
         sum0 = [keep.tile([P, HALF], F32, name=f"sum0{h}") for h in range(2)]
         result0 = [keep.tile([P, HALF], F32, name=f"result0{h}") for h in range(2)]

@@ -38,13 +38,8 @@ def tile_picked_spconv_relu_e_kernel(
         w_scales = [keep.tile([P, N], U8, name=f"w_scales{d}", align_bytes=64) for d in range(2)]
         spread = [[keep.tile([P, U], F32, name=f"spread{d}{b}") for b in range(2)] for d in range(2)]
 
-        zero = keep.tile([P, 1], F32, name="zero")
-        zero_bias = keep.tile([P, 1], F32, name="zero_bias")
-
         for d in range(2):
             nc.gpsimd.memset(w_scales[d][:].bitcast(I32), 0)
-        nc.vector.memset(zero[:], 0.0)
-        nc.scalar.activation(zero_bias[:], zero[:], RELU)
 
         x_rows = xT.rearrange("(p j) t -> j p t", j=PACK)
 
@@ -106,6 +101,8 @@ def tile_picked_spconv_relu_e_kernel(
         banks = [psum.tile([P, U], F32, name=f"bank{i}") for i in range(6)]
 
         PIECE = V // 2
+        FIRST = PIECE // 2
+        LAST = PACK - 1
         cuts = [(0, PIECE), (PIECE, V)]
         woven_a = keep.tile([P, PIECE * PACK], BF16, name="woven_a", tag="turns", align_bytes=64)
         woven_b = keep.tile([P, PIECE * PACK], BF16, name="woven_b", align_bytes=64)
@@ -116,38 +113,46 @@ def tile_picked_spconv_relu_e_kernel(
             c0, c1 = cuts[i]
             nc.vector.tensor_copy(plane(woven0[i], j, 0, PIECE), rows[j][:].indirect(offsets(0, c0, c1)))
 
-        rounded = [keep.tile([P, T], BF16, name=f"rounded{j}") for j in range(PACK - 1)]
+        def gather1(j, rounded):
+            nc.scalar.activation(plane(woven1, j, 0, V), rounded[:].indirect(offsets(1, 0, V)), COPY)
 
-        for j in range(PACK - 1):
+        for j in range(LAST):
             for i in range(2):
                 gather0(i, j)
+            rounded = keep.tile([P, T], BF16, name=f"rounded{j}")
             if j == 0:
-                nc.scalar.copy(rounded[j][:], rows[j][:])
+                nc.scalar.copy(rounded[:], rows[j][:])
             else:
-                nc.gpsimd.tensor_copy(rounded[j][:], rows[j][:])
-            nc.scalar.activation(plane(woven1, j, 0, V), rounded[j][:].indirect(offsets(1, 0, V)), COPY)
+                nc.gpsimd.tensor_copy(rounded[:], rows[j][:])
+            gather1(j, rounded)
 
-        LAST = PACK - 1
         for i in range(2):
             gather0(i, LAST)
-        for i, (c0, c1) in enumerate(cuts):
-            quantise(0, woven0[i][:], c0, c1)
-            for b in range(2):
-                product(0, b, c0, c1, banks[2 * i + b][:, 0:PIECE])
+        y_first = keep.tile([P, FIRST], F32, name="y_first")
+        y_second = keep.tile([P, PIECE], F32, name="y_second")
+
+        quantise(0, woven_a[:, 0 : FIRST * PACK], 0, FIRST)
+        product(0, 0, 0, FIRST, banks[0][:, 0:FIRST])
+        nc.scalar.copy(y_first[:], banks[0][:, 0:FIRST])
+        quantise(0, woven_a[:, FIRST * PACK : PIECE * PACK], FIRST, PIECE)
+        product(0, 1, 0, PIECE, banks[1][:, 0:PIECE])
+        nc.scalar.copy(y_second[:], banks[1][:, 0:PIECE])
+        quantise(0, woven_b[:], PIECE, V)
+        product(0, 0, FIRST, PIECE, banks[2][:, FIRST:PIECE])
+        product(0, 0, PIECE, V, banks[2][:, PIECE:V])
+        product(0, 1, PIECE, V, banks[3][:, PIECE:V])
         picked = keep.tile([P, V], F32, name="picked", tag="turns", align_bytes=64)
         nc.vector.tensor_copy(picked[:], rows[LAST][:].indirect(offsets(1, 0, V)))
+        scatter(0, 0, 0, FIRST, y_first[:])
+        scatter(0, 1, 0, PIECE, y_second[:])
 
-        def put(i, b, y):
-            c0, c1 = cuts[i]
-            nc.scalar.copy(y[:], banks[2 * i + b][:, 0:PIECE])
-            scatter(0, b, c0, c1, y[:])
-
-        for b in range(2):
-            put(0, b, keep.tile([P, PIECE], F32, name=f"y0{b}"))
         nc.scalar.copy(plane(woven1, LAST, 0, V), picked[:])
         quantise(1, woven1[:], 0, V)
-        put(1, 0, keep.tile([P, PIECE], F32, name="y10", tag="turns", align_bytes=64))
-        put(1, 1, keep.tile([P, PIECE], F32, name="y11"))
+        y_late = keep.tile([P, V - FIRST + PIECE], F32, name="y_late", tag="turns", align_bytes=64)
+        nc.scalar.copy(y_late[:, 0 : V - FIRST], banks[2][:, FIRST:V])
+        nc.scalar.copy(y_late[:, V - FIRST : V - FIRST + PIECE], banks[3][:, PIECE:V])
+        scatter(0, 0, FIRST, V, y_late[:, 0 : V - FIRST])
+        scatter(0, 1, PIECE, V, y_late[:, V - FIRST : V - FIRST + PIECE])
         for b in range(2):
             product(1, b, 0, V, banks[4 + b][:, 0:V])
             y = keep.tile([P, V], F32, name=f"y_tap1{b}")
@@ -159,7 +164,7 @@ def tile_picked_spconv_relu_e_kernel(
         for h in range(2):
             cols = slice(h * HALF, (h + 1) * HALF)
             nc.gpsimd.tensor_tensor(sum0[h][:], spread[0][0][:, cols], spread[1][0][:, cols], ADD)
-            nc.scalar.activation(result0[h][:], sum0[h][:], RELU, bias=zero_bias[:])
+            nc.scalar.activation(result0[h][:], sum0[h][:], RELU)
             nc.scalar.dma_start(out[0:P, cols], result0[h][:])
         late = sum0[1][:]
 
@@ -168,7 +173,7 @@ def tile_picked_spconv_relu_e_kernel(
         for h in range(2):
             cols = slice(h * HALF, (h + 1) * HALF)
             nc.vector.tensor_tensor(total[h][:], spread[0][1][:, cols], spread[1][1][:, cols], ADD)
-        nc.scalar.activation(late, total[0][:], RELU, bias=zero_bias[:])
+        nc.scalar.activation(late, total[0][:], RELU)
         nc.scalar.dma_start(out[P : 2 * P, 0:HALF], late)
         nc.vector.tensor_scalar_max(result1[:], total[1][:], 0.0)
         nc.sync.dma_start(out[P : 2 * P, HALF:U], result1[:])

@@ -140,7 +140,6 @@ def tile_picked_spconv_relu_e_kernel(
         quantise(0, woven_b[:], PIECE, V)
         product(0, 0, FIRST, PIECE, banks[2][:, FIRST:PIECE])
         product(0, 0, PIECE, V, banks[2][:, PIECE:V])
-        product(0, 1, PIECE, V, banks[3][:, PIECE:V])
         picked = keep.tile([P, V], F32, name="picked", tag="turns", align_bytes=64)
         nc.vector.tensor_copy(picked[:], rows[LAST][:].indirect(offsets(1, 0, V)))
         scatter(0, 0, 0, FIRST, y_first[:])
@@ -148,32 +147,40 @@ def tile_picked_spconv_relu_e_kernel(
 
         nc.scalar.copy(plane(woven1, LAST, 0, V), picked[:])
         quantise(1, woven1[:], 0, V)
-        y_late = keep.tile([P, V - FIRST + PIECE], F32, name="y_late", tag="turns", align_bytes=64)
-        nc.scalar.copy(y_late[:, 0 : V - FIRST], banks[2][:, FIRST:V])
-        nc.scalar.copy(y_late[:, V - FIRST : V - FIRST + PIECE], banks[3][:, PIECE:V])
-        scatter(0, 0, FIRST, V, y_late[:, 0 : V - FIRST])
-        scatter(0, 1, PIECE, V, y_late[:, V - FIRST : V - FIRST + PIECE])
-        for b in range(2):
-            product(1, b, 0, V, banks[4 + b][:, 0:V])
-            y = keep.tile([P, V], F32, name=f"y_tap1{b}")
-            nc.scalar.copy(y[:], banks[4 + b][:, 0:V])
-            scatter(1, b, 0, V, y[:])
+        y_third = keep.tile([P, V - FIRST], F32, name="y_third", tag="turns", align_bytes=64)
+        nc.scalar.copy(y_third[:], banks[2][:, FIRST:V])
+        scatter(0, 0, FIRST, V, y_third[:])
 
-        sum0 = [keep.tile([P, HALF], F32, name=f"sum0{h}") for h in range(2)]
+        y_tap1 = [keep.tile([P, V], F32, name=f"y_tap1{b}") for b in range(2)]
+        y_fourth = keep.tile([P, PIECE], F32, name="y_fourth")
+        product(1, 0, 0, V, banks[3][:, 0:V])
+        nc.scalar.copy(y_tap1[0][:], banks[3][:, 0:V])
+        scatter(1, 0, 0, V, y_tap1[0][:])
+        product(0, 1, PIECE, V, banks[3][:, 0:PIECE])
+        nc.scalar.copy(y_fourth[:], banks[3][:, 0:PIECE])
+        scatter(0, 1, PIECE, V, y_fourth[:])
+        product(1, 1, 0, V, banks[4][:, 0:V])
+        nc.scalar.copy(y_tap1[1][:], banks[4][:, 0:V])
+        scatter(1, 1, 0, V, y_tap1[1][:])
+
+        sum0 = [keep.tile([P, HALF], F32, name="sum00"), keep.tile([P, HALF], F32, name="sum01", tag="late")]
         result0 = [keep.tile([P, HALF], F32, name=f"result0{h}") for h in range(2)]
         for h in range(2):
             cols = slice(h * HALF, (h + 1) * HALF)
             nc.gpsimd.tensor_tensor(sum0[h][:], spread[0][0][:, cols], spread[1][0][:, cols], ADD)
             nc.scalar.activation(result0[h][:], sum0[h][:], RELU)
             nc.scalar.dma_start(out[0:P, cols], result0[h][:])
-        late = sum0[1][:]
 
-        total = [keep.tile([P, HALF], F32, name=f"total{h}") for h in range(2)]
-        result1 = keep.tile([P, HALF], F32, name="result1")
-        for h in range(2):
-            cols = slice(h * HALF, (h + 1) * HALF)
+        SPLIT = 320
+        shares = [slice(0, SPLIT), slice(SPLIT, U)]
+        total = [keep.tile([P, c.stop - c.start], F32, name=f"total{c.start}") for c in shares]
+        result1 = [
+            keep.tile([P, SPLIT], F32, name="result10", tag="late"),
+            keep.tile([P, U - SPLIT], F32, name="result11"),
+        ]
+        for h, cols in enumerate(shares):
             nc.vector.tensor_tensor(total[h][:], spread[0][1][:, cols], spread[1][1][:, cols], ADD)
-        nc.scalar.activation(late, total[0][:], RELU)
-        nc.scalar.dma_start(out[P : 2 * P, 0:HALF], late)
-        nc.vector.tensor_scalar_max(result1[:], total[1][:], 0.0)
-        nc.sync.dma_start(out[P : 2 * P, HALF:U], result1[:])
+        nc.scalar.activation(result1[0][:], total[0][:], RELU)
+        nc.scalar.dma_start(out[P : 2 * P, shares[0]], result1[0][:])
+        nc.vector.tensor_scalar_max(result1[1][:], total[1][:], 0.0)
+        nc.sync.dma_start(out[P : 2 * P, shares[1]], result1[1][:])

@@ -98,7 +98,7 @@ def tile_picked_spconv_relu_e_kernel(
         def scatter(d, b, c0, c1, y):
             nc.vector.tensor_copy(spread[d][b][:].indirect(places[d][:, c0 // GROUP : c1 // GROUP]), y)
 
-        banks = [psum.tile([P, U], F32, name=f"bank{i}") for i in range(6)]
+        banks = [psum.tile([P, U], F32, name=f"bank{i}") for i in range(7)]
 
         PIECE = V // 2
         FIRST = PIECE // 2
@@ -137,28 +137,34 @@ def tile_picked_spconv_relu_e_kernel(
         quantise(0, woven_a[:, FIRST * PACK : PIECE * PACK], FIRST, PIECE)
         product(0, 1, 0, PIECE, banks[1][:, 0:PIECE])
         nc.scalar.copy(y_second[:], banks[1][:, 0:PIECE])
+        y_third = keep.tile([P, FIRST], F32, name="y_third")
+        product(0, 0, FIRST, PIECE, banks[2][:, 0:FIRST])
+        nc.scalar.copy(y_third[:], banks[2][:, 0:FIRST])
         quantise(0, woven_b[:], PIECE, V)
-        product(0, 0, FIRST, PIECE, banks[2][:, FIRST:PIECE])
-        product(0, 0, PIECE, V, banks[2][:, PIECE:V])
+        product(0, 0, PIECE, V, banks[5][:, 0:PIECE])
+        product(0, 1, PIECE, PIECE + FIRST, banks[5][:, PIECE : PIECE + FIRST])
         picked = keep.tile([P, V], F32, name="picked", tag="turns", align_bytes=64)
         nc.vector.tensor_copy(picked[:], rows[LAST][:].indirect(offsets(1, 0, V)))
         scatter(0, 0, 0, FIRST, y_first[:])
         scatter(0, 1, 0, PIECE, y_second[:])
+        scatter(0, 0, FIRST, PIECE, y_third[:])
 
         nc.scalar.copy(plane(woven1, LAST, 0, V), picked[:])
         quantise(1, woven1[:], 0, V)
-        y_third = keep.tile([P, V - FIRST], F32, name="y_third", tag="turns", align_bytes=64)
-        nc.scalar.copy(y_third[:], banks[2][:, FIRST:V])
-        scatter(0, 0, FIRST, V, y_third[:])
+        y_late = keep.tile([P, PIECE + FIRST], F32, name="y_late", tag="turns", align_bytes=64)
+        nc.scalar.copy(y_late[:], banks[5][:, 0 : PIECE + FIRST])
+        scatter(0, 0, PIECE, V, y_late[:, 0:PIECE])
+        scatter(0, 1, PIECE, PIECE + FIRST, y_late[:, PIECE : PIECE + FIRST])
 
         y_tap1 = [keep.tile([P, V], F32, name=f"y_tap1{b}") for b in range(2)]
-        y_fourth = keep.tile([P, PIECE], F32, name="y_fourth")
-        product(1, 0, 0, V, banks[3][:, 0:V])
-        nc.scalar.copy(y_tap1[0][:], banks[3][:, 0:V])
+        y_last = keep.tile([P, FIRST], F32, name="y_last")
+        for i, (c0, c1) in enumerate(cuts):
+            product(1, 0, c0, c1, banks[3 + 3 * i][:, 0:PIECE])
+            nc.scalar.copy(y_tap1[0][:, c0:c1], banks[3 + 3 * i][:, 0:PIECE])
         scatter(1, 0, 0, V, y_tap1[0][:])
-        product(0, 1, PIECE, V, banks[3][:, 0:PIECE])
-        nc.scalar.copy(y_fourth[:], banks[3][:, 0:PIECE])
-        scatter(0, 1, PIECE, V, y_fourth[:])
+        product(0, 1, V - FIRST, V, banks[6][:, 0:FIRST])
+        nc.scalar.copy(y_last[:], banks[6][:, 0:FIRST])
+        scatter(0, 1, V - FIRST, V, y_last[:])
         product(1, 1, 0, V, banks[4][:, 0:V])
         nc.scalar.copy(y_tap1[1][:], banks[4][:, 0:V])
         scatter(1, 1, 0, V, y_tap1[1][:])

@@ -169,7 +169,7 @@ def tile_picked_spconv_relu_e_kernel(
         nc.scalar.copy(y_tap1[1][:], banks[4][:, 0:V])
         scatter(1, 1, 0, V, y_tap1[1][:])
 
-        sum0 = [keep.tile([P, HALF], F32, name="sum00"), keep.tile([P, HALF], F32, name="sum01", tag="late")]
+        sum0 = [keep.tile([P, HALF], F32, name=f"sum0{h}") for h in range(2)]
         result0 = [keep.tile([P, HALF], F32, name=f"result0{h}") for h in range(2)]
         for h in range(2):
             cols = slice(h * HALF, (h + 1) * HALF)
@@ -177,16 +177,11 @@ def tile_picked_spconv_relu_e_kernel(
             nc.scalar.activation(result0[h][:], sum0[h][:], RELU)
             nc.scalar.dma_start(out[0:P, cols], result0[h][:])
 
-        SPLIT = 320
-        shares = [slice(0, SPLIT), slice(SPLIT, U)]
+        edges = [0, 192, 384, 512]
+        shares = [slice(a, b) for a, b in zip(edges[:-1], edges[1:])]
         total = [keep.tile([P, c.stop - c.start], F32, name=f"total{c.start}") for c in shares]
-        result1 = [
-            keep.tile([P, SPLIT], F32, name="result10", tag="late"),
-            keep.tile([P, U - SPLIT], F32, name="result11"),
-        ]
+        result1 = [keep.tile([P, c.stop - c.start], F32, name=f"result1{c.start}") for c in shares]
         for h, cols in enumerate(shares):
             nc.vector.tensor_tensor(total[h][:], spread[0][1][:, cols], spread[1][1][:, cols], ADD)
-        nc.scalar.activation(result1[0][:], total[0][:], RELU)
-        nc.scalar.dma_start(out[P : 2 * P, shares[0]], result1[0][:])
-        nc.vector.tensor_scalar_max(result1[1][:], total[1][:], 0.0)
-        nc.sync.dma_start(out[P : 2 * P, shares[1]], result1[1][:])
+            nc.vector.tensor_scalar_max(result1[h][:], total[h][:], 0.0)
+            nc.sync.dma_start(out[P : 2 * P, cols], result1[h][:])

@@ -126,8 +126,9 @@ def tile_picked_spconv_relu_e_kernel(
                 nc.gpsimd.tensor_copy(rounded[:], rows[j][:])
             gather1(j, rounded)
 
-        for i in range(2):
-            gather0(i, LAST)
+        gather0(0, LAST)
+        picked_b = keep.tile([P, PIECE], F32, name="picked_b")
+        nc.vector.tensor_copy(picked_b[:], rows[LAST][:].indirect(offsets(0, PIECE, V)))
         y_first = keep.tile([P, FIRST], F32, name="y_first")
         y_second = keep.tile([P, PIECE], F32, name="y_second")
 
@@ -140,6 +141,7 @@ def tile_picked_spconv_relu_e_kernel(
         y_third = keep.tile([P, FIRST], F32, name="y_third")
         product(0, 0, FIRST, PIECE, banks[2][:, 0:FIRST])
         nc.scalar.copy(y_third[:], banks[2][:, 0:FIRST])
+        nc.vector.tensor_copy(plane(woven_b, LAST, 0, PIECE), picked_b[:])
         quantise(0, woven_b[:], PIECE, V)
         product(0, 0, PIECE, V, banks[5][:, 0:PIECE])
         product(0, 1, PIECE, PIECE + FIRST, banks[5][:, PIECE : PIECE + FIRST])
@@ -183,5 +185,6 @@ def tile_picked_spconv_relu_e_kernel(
         result1 = [keep.tile([P, c.stop - c.start], F32, name=f"result1{c.start}") for c in shares]
         for h, cols in enumerate(shares):
             nc.vector.tensor_tensor(total[h][:], spread[0][1][:, cols], spread[1][1][:, cols], ADD)
+        for h, cols in enumerate(shares):
             nc.vector.tensor_scalar_max(result1[h][:], total[h][:], 0.0)
             nc.sync.dma_start(out[P : 2 * P, cols], result1[h][:])

@@ -104,7 +104,7 @@ def tile_picked_spconv_relu_e_kernel(
         FIRST = PIECE // 2
         LAST = PACK - 1
         cuts = [(0, PIECE), (PIECE, V)]
-        woven_a = keep.tile([P, PIECE * PACK], BF16, name="woven_a", tag="turns", align_bytes=64)
+        woven_a = keep.tile([P, PIECE * PACK], BF16, name="woven_a", align_bytes=64)
         woven_b = keep.tile([P, PIECE * PACK], BF16, name="woven_b", align_bytes=64)
         woven0 = [woven_a, woven_b]
         woven1 = keep.tile([P, V * PACK], BF16, name="woven1", align_bytes=64)
@@ -122,13 +122,16 @@ def tile_picked_spconv_relu_e_kernel(
             rounded = keep.tile([P, T], BF16, name=f"rounded{j}")
             if j == 0:
                 nc.scalar.copy(rounded[:], rows[j][:])
-            else:
+            elif j == 1:
                 nc.gpsimd.tensor_copy(rounded[:], rows[j][:])
+            else:
+                nc.scalar.copy(rounded[:, 0 : T // 2], rows[j][:, 0 : T // 2])
+                nc.gpsimd.tensor_copy(rounded[:, T // 2 : T], rows[j][:, T // 2 : T])
             gather1(j, rounded)
 
         gather0(0, LAST)
-        picked_b = keep.tile([P, PIECE], F32, name="picked_b")
-        nc.vector.tensor_copy(picked_b[:], rows[LAST][:].indirect(offsets(0, PIECE, V)))
+        rounded = keep.tile([P, T], BF16, name="rounded_last")
+        nc.vector.tensor_copy(rounded[:, 0 : T // 2], rows[LAST][:, 0 : T // 2])
         y_first = keep.tile([P, FIRST], F32, name="y_first")
         y_second = keep.tile([P, PIECE], F32, name="y_second")
 
@@ -138,25 +141,22 @@ def tile_picked_spconv_relu_e_kernel(
         quantise(0, woven_a[:, FIRST * PACK : PIECE * PACK], FIRST, PIECE)
         product(0, 1, 0, PIECE, banks[1][:, 0:PIECE])
         nc.scalar.copy(y_second[:], banks[1][:, 0:PIECE])
-        y_third = keep.tile([P, FIRST], F32, name="y_third")
-        product(0, 0, FIRST, PIECE, banks[2][:, 0:FIRST])
-        nc.scalar.copy(y_third[:], banks[2][:, 0:FIRST])
-        nc.vector.tensor_copy(plane(woven_b, LAST, 0, PIECE), picked_b[:])
+        product(0, 0, FIRST, PIECE, banks[5][:, 0:FIRST])
+        gather0(1, LAST)
+        nc.vector.tensor_copy(rounded[:, T // 2 : T], rows[LAST][:, T // 2 : T])
         quantise(0, woven_b[:], PIECE, V)
-        product(0, 0, PIECE, V, banks[5][:, 0:PIECE])
-        product(0, 1, PIECE, PIECE + FIRST, banks[5][:, PIECE : PIECE + FIRST])
-        picked = keep.tile([P, V], F32, name="picked", tag="turns", align_bytes=64)
-        nc.vector.tensor_copy(picked[:], rows[LAST][:].indirect(offsets(1, 0, V)))
+        product(0, 0, PIECE, V, banks[5][:, FIRST : FIRST + PIECE])
+        product(0, 1, PIECE, PIECE + FIRST, banks[5][:, FIRST + PIECE : V])
+        gather1(LAST, rounded)
         scatter(0, 0, 0, FIRST, y_first[:])
         scatter(0, 1, 0, PIECE, y_second[:])
-        scatter(0, 0, FIRST, PIECE, y_third[:])
 
-        nc.scalar.copy(plane(woven1, LAST, 0, V), picked[:])
         quantise(1, woven1[:], 0, V)
-        y_late = keep.tile([P, PIECE + FIRST], F32, name="y_late", tag="turns", align_bytes=64)
-        nc.scalar.copy(y_late[:], banks[5][:, 0 : PIECE + FIRST])
-        scatter(0, 0, PIECE, V, y_late[:, 0:PIECE])
-        scatter(0, 1, PIECE, PIECE + FIRST, y_late[:, PIECE : PIECE + FIRST])
+        y_late = keep.tile([P, V], F32, name="y_late")
+        nc.scalar.copy(y_late[:, 0 : FIRST + PIECE], banks[5][:, 0 : FIRST + PIECE])
+        nc.scalar.copy(y_late[:, FIRST + PIECE : V], banks[5][:, FIRST + PIECE : V])
+        scatter(0, 0, FIRST, V, y_late[:, 0 : FIRST + PIECE])
+        scatter(0, 1, PIECE, PIECE + FIRST, y_late[:, FIRST + PIECE : V])
 
         y_tap1 = [keep.tile([P, V], F32, name=f"y_tap1{b}") for b in range(2)]
         y_last = keep.tile([P, FIRST], F32, name="y_last")

@@ -179,12 +179,17 @@ def tile_picked_spconv_relu_e_kernel(
             nc.scalar.activation(result0[h][:], sum0[h][:], RELU)
             nc.scalar.dma_start(out[0:P, cols], result0[h][:])
 
-        edges = [0, 192, 384, 512]
+        edges = [0, 128, 384, 512]
         shares = [slice(a, b) for a, b in zip(edges[:-1], edges[1:])]
         total = [keep.tile([P, c.stop - c.start], F32, name=f"total{c.start}") for c in shares]
         result1 = [keep.tile([P, c.stop - c.start], F32, name=f"result1{c.start}") for c in shares]
+
+        def add(h):
+            nc.vector.tensor_tensor(total[h][:], spread[0][1][:, shares[h]], spread[1][1][:, shares[h]], ADD)
+
+        add(0)
         for h, cols in enumerate(shares):
-            nc.vector.tensor_tensor(total[h][:], spread[0][1][:, cols], spread[1][1][:, cols], ADD)
-        for h, cols in enumerate(shares):
+            if h + 1 < len(shares):
+                add(h + 1)
             nc.vector.tensor_scalar_max(result1[h][:], total[h][:], 0.0)
             nc.sync.dma_start(out[P : 2 * P, cols], result1[h][:])

@@ -146,27 +146,25 @@ def tile_picked_spconv_relu_e_kernel(
         nc.vector.tensor_copy(rounded[:, T // 2 : T], rows[LAST][:, T // 2 : T])
         quantise(0, woven_b[:], PIECE, V)
         product(0, 0, PIECE, V, banks[5][:, FIRST : FIRST + PIECE])
-        product(0, 1, PIECE, PIECE + FIRST, banks[5][:, FIRST + PIECE : V])
         gather1(LAST, rounded)
         scatter(0, 0, 0, FIRST, y_first[:])
         scatter(0, 1, 0, PIECE, y_second[:])
 
-        quantise(1, woven1[:], 0, V)
-        y_late = keep.tile([P, V], F32, name="y_late")
+        for c0, c1 in cuts:
+            quantise(1, woven1[:, c0 * PACK : c1 * PACK], c0, c1)
+        y_late = keep.tile([P, FIRST + PIECE], F32, name="y_late")
         nc.scalar.copy(y_late[:, 0 : FIRST + PIECE], banks[5][:, 0 : FIRST + PIECE])
-        nc.scalar.copy(y_late[:, FIRST + PIECE : V], banks[5][:, FIRST + PIECE : V])
         scatter(0, 0, FIRST, V, y_late[:, 0 : FIRST + PIECE])
-        scatter(0, 1, PIECE, PIECE + FIRST, y_late[:, FIRST + PIECE : V])
 
         y_tap1 = [keep.tile([P, V], F32, name=f"y_tap1{b}") for b in range(2)]
-        y_last = keep.tile([P, FIRST], F32, name="y_last")
+        y_last = keep.tile([P, PIECE], F32, name="y_last")
         for i, (c0, c1) in enumerate(cuts):
             product(1, 0, c0, c1, banks[3 + 3 * i][:, 0:PIECE])
             nc.scalar.copy(y_tap1[0][:, c0:c1], banks[3 + 3 * i][:, 0:PIECE])
         scatter(1, 0, 0, V, y_tap1[0][:])
-        product(0, 1, V - FIRST, V, banks[6][:, 0:FIRST])
-        nc.scalar.copy(y_last[:], banks[6][:, 0:FIRST])
-        scatter(0, 1, V - FIRST, V, y_last[:])
+        product(0, 1, PIECE, V, banks[6][:, 0:PIECE])
+        nc.scalar.copy(y_last[:], banks[6][:, 0:PIECE])
+        scatter(0, 1, PIECE, V, y_last[:])
         product(1, 1, 0, V, banks[4][:, 0:V])
         nc.scalar.copy(y_tap1[1][:], banks[4][:, 0:V])
         scatter(1, 1, 0, V, y_tap1[1][:])

@@ -16,6 +16,7 @@ COPY = mybir.ActivationFunctionType.Copy
 RELU = mybir.ActivationFunctionType.Relu
 ADD = mybir.AluOpType.add
 MULT = mybir.AluOpType.mult
+MAX = mybir.AluOpType.max
 
 P = 128
 PACK = 4
@@ -46,42 +47,44 @@ def tile_picked_spconv_relu_e_kernel(
         def load_words(d, words):
             nc.sync.dma_start(w_codes[d][:].bitcast(I32), words[0].rearrange("p n r -> p (n r)").bitcast(I32))
 
-        def load_scales(engine, d, scales, quadrants):
-            for q in quadrants:
+        def load_scales(engine, d, scales):
+            for q in range(4):
                 engine.dma_start(
                     w_scales[d][32 * q : 32 * q + 4, :].bitcast(I32), scales[0, 4 * q : 4 * q + 4, :].bitcast(I32)
                 )
 
-        load_scales(nc.scalar, 0, w1_scales, range(4))
+        load_scales(nc.gpsimd, 1, w2_scales)
         nc.sync.dma_start(rows[0][:], x_rows[0])
         nc.sync.dma_start(picks[:], offs)
+        nc.sync.dma_start(places[0][:], to1)
+        nc.sync.dma_start(places[1][:], to2)
         for j in range(1, PACK):
             nc.sync.dma_start(rows[j][:], x_rows[j])
-        load_words(0, w1_words)
-        nc.sync.dma_start(places[0][:], to1)
         load_words(1, w2_words)
-        load_scales(nc.sync, 1, w2_scales, range(4))
-        nc.sync.dma_start(places[1][:], to2)
+        load_words(0, w1_words)
+        load_scales(nc.sync, 0, w1_scales)
 
-        for d in range(2):
-            for b in range(2):
-                nc.vector.memset(spread[d][b][:], 0.0)
+        for d, b in ((0, 0), (0, 1), (1, 0)):
+            nc.vector.memset(spread[d][b][:], 0.0)
+        nc.scalar.activation(spread[1][1][:], spread[0][0][:], COPY)
 
-        x_codes = [keep.tile([P, V], U32, name=f"x_codes{d}", align_bytes=64) for d in range(2)]
-        x_scales = [keep.tile([P, V], U8, name=f"x_scales{d}", align_bytes=64) for d in range(2)]
+        SHIFT = 192
+        x_codes = keep.tile([P, S], U32, name="x_codes", align_bytes=64)
+        x_scales = keep.tile([P, S], U8, name="x_scales", align_bytes=64)
 
-        def offsets(d, c0, c1):
-            return picks[:, (d * V + c0) // GROUP : (d * V + c1) // GROUP]
+        def offsets(c0, c1):
+            e0 = (c0 + SHIFT) % S
+            return picks[:, e0 // GROUP : (e0 + c1 - c0) // GROUP]
 
-        def plane(woven, j, c0, c1):
-            return woven[:].rearrange("p (c j) -> p c j", j=PACK)[:, c0:c1, j]
+        PIECE = 128
+        woven = [keep.tile([P, PIECE * PACK], BF16, name=f"woven{i}", align_bytes=64) for i in range(4)]
 
-        def quantise(d, woven, c0, c1):
-            nc.vector.quantize_mx(
-                out=x_codes[d][:, c0:c1].bitcast(FP8X4),
-                scales=x_scales[d][:, c0:c1],
-                in_=woven,
-            )
+        def lanes(i):
+            return woven[i][:].rearrange("p (c j) -> p c j", j=PACK)
+
+        def quantise(i):
+            cols = slice(i * PIECE, (i + 1) * PIECE)
+            nc.vector.quantize_mx(out=x_codes[:, cols].bitcast(FP8X4), scales=x_scales[:, cols], in_=woven[i][:])
 
         def product(d, b, c0, c1, acc):
             m_cols = slice(b * P, (b + 1) * P)
@@ -89,97 +92,91 @@ def tile_picked_spconv_relu_e_kernel(
                 out=acc,
                 lhsT=w_codes[d][:, m_cols].bitcast(FP8X4),
                 lhsT_scale=w_scales[d][:, m_cols],
-                rhs=x_codes[d][:, c0:c1].bitcast(FP8X4),
-                rhs_scale=x_scales[d][:, c0:c1],
+                rhs=x_codes[:, c0:c1].bitcast(FP8X4),
+                rhs_scale=x_scales[:, c0:c1],
                 start=True,
                 stop=True,
             )
 
-        def scatter(d, b, c0, c1, y):
-            nc.vector.tensor_copy(spread[d][b][:].indirect(places[d][:, c0 // GROUP : c1 // GROUP]), y)
+        def gather_woven(i, j):
+            nc.vector.tensor_copy(lanes(i)[:, :, j], rows[j][:].indirect(offsets(i * PIECE, (i + 1) * PIECE)))
 
-        banks = [psum.tile([P, U], F32, name=f"bank{i}") for i in range(7)]
+        def gather_plain(dst, j, c0, c1):
+            nc.scalar.activation(dst, rows[j][:].indirect(offsets(c0, c1)), COPY)
 
-        PIECE = V // 2
-        FIRST = PIECE // 2
-        LAST = PACK - 1
-        cuts = [(0, PIECE), (PIECE, V)]
-        woven_a = keep.tile([P, PIECE * PACK], BF16, name="woven_a", align_bytes=64)
-        woven_b = keep.tile([P, PIECE * PACK], BF16, name="woven_b", align_bytes=64)
-        woven0 = [woven_a, woven_b]
-        woven1 = keep.tile([P, V * PACK], BF16, name="woven1", align_bytes=64)
+        low = keep.tile([P, 2, 2 * PIECE], BF16, name="low")
+        high = [None] + [keep.tile([P, 2, PIECE], BF16, name=f"high{i}") for i in range(1, 3)]
 
-        def gather0(i, j):
-            c0, c1 = cuts[i]
-            nc.vector.tensor_copy(plane(woven0[i], j, 0, PIECE), rows[j][:].indirect(offsets(0, c0, c1)))
+        for j in range(2):
+            gather_woven(0, j)
+            gather_woven(3, j)
+            gather_plain(low[:, j, 0:192], j, 128, 320)
+            gather_plain(low[:, j, 192:256], j, 320, 384)
+        for i in range(1, 3):
+            nc.vector.tensor_copy(
+                lanes(i)[:, :, 0:2], low[:, :, (i - 1) * PIECE : i * PIECE].rearrange("p j c -> p c j")
+            )
+        for j in range(2, 4):
+            gather_woven(0, j)
+            gather_woven(3, j)
+            gather_plain(high[1][:, j - 2, :], j, 128, 256)
+            gather_plain(high[2][:, j - 2, 0:64], j, 256, 320)
+            gather_plain(high[2][:, j - 2, 64:128], j, 320, 384)
 
-        def gather1(j, rounded):
-            nc.scalar.activation(plane(woven1, j, 0, V), rounded[:].indirect(offsets(1, 0, V)), COPY)
+        def weave(engine_copy, i):
+            engine_copy(lanes(i)[:, :, 2:4], high[i][:].rearrange("p j c -> p c j"))
 
-        for j in range(LAST):
-            for i in range(2):
-                gather0(i, j)
-            rounded = keep.tile([P, T], BF16, name=f"rounded{j}")
-            if j == 0:
-                nc.scalar.copy(rounded[:], rows[j][:])
-            elif j == 1:
-                nc.gpsimd.tensor_copy(rounded[:], rows[j][:])
-            else:
-                nc.scalar.copy(rounded[:, 0 : T // 2], rows[j][:, 0 : T // 2])
-                nc.gpsimd.tensor_copy(rounded[:, T // 2 : T], rows[j][:, T // 2 : T])
-            gather1(j, rounded)
+        banks = [psum.tile([P, U], F32, name=f"bank{i}") for i in range(2)]
+        y_rest = keep.tile([P, 2, 192], F32, name="y_rest")
+        y_late = [keep.tile([P, V], F32, name=f"y_late{d}") for d in range(2)]
 
-        gather0(0, LAST)
-        rounded = keep.tile([P, T], BF16, name="rounded_last")
-        nc.vector.tensor_copy(rounded[:, 0 : T // 2], rows[LAST][:, 0 : T // 2])
-        y_first = keep.tile([P, FIRST], F32, name="y_first")
-        y_second = keep.tile([P, PIECE], F32, name="y_second")
+        def scatter_v(d, b, v0, v1, y):
+            nc.vector.tensor_copy(spread[d][b][:].indirect(places[d][:, v0 // GROUP : v1 // GROUP]), y)
 
-        quantise(0, woven_a[:, 0 : FIRST * PACK], 0, FIRST)
-        product(0, 0, 0, FIRST, banks[0][:, 0:FIRST])
-        nc.scalar.copy(y_first[:], banks[0][:, 0:FIRST])
-        quantise(0, woven_a[:, FIRST * PACK : PIECE * PACK], FIRST, PIECE)
-        product(0, 1, 0, PIECE, banks[1][:, 0:PIECE])
-        nc.scalar.copy(y_second[:], banks[1][:, 0:PIECE])
-        product(0, 0, FIRST, PIECE, banks[5][:, 0:FIRST])
-        gather0(1, LAST)
-        nc.vector.tensor_copy(rounded[:, T // 2 : T], rows[LAST][:, T // 2 : T])
-        quantise(0, woven_b[:], PIECE, V)
-        product(0, 0, PIECE, V, banks[5][:, FIRST : FIRST + PIECE])
-        gather1(LAST, rounded)
-        scatter(0, 0, 0, FIRST, y_first[:])
-        scatter(0, 1, 0, PIECE, y_second[:])
+        def scatter_s(d, b, v0, v1, y):
+            nc.scalar.activation(spread[d][b][:].indirect(places[d][:, v0 // GROUP : v1 // GROUP]), y, COPY)
 
-        for c0, c1 in cuts:
-            quantise(1, woven1[:, c0 * PACK : c1 * PACK], c0, c1)
-        y_late = keep.tile([P, FIRST + PIECE], F32, name="y_late")
-        nc.scalar.copy(y_late[:, 0 : FIRST + PIECE], banks[5][:, 0 : FIRST + PIECE])
-        scatter(0, 0, FIRST, V, y_late[:, 0 : FIRST + PIECE])
+        quantise(0)
+        product(1, 0, 64, 128, banks[0][:, 64:128])
+        product(0, 0, 0, 64, banks[0][:, 0:64])
+        weave(nc.scalar.copy, 2)
+        nc.scalar.copy(y_rest[:, :, 0:64], banks[0][:, 0:128].rearrange("p (d c) -> p d c", d=2))
+        quantise(3)
+        product(0, 0, 384, 512, banks[1][:, 64:192])
+        weave(nc.vector.tensor_copy, 1)
+        quantise(2)
+        quantise(1)
+        product(0, 0, 320, 384, banks[1][:, 0:64])
+        product(1, 0, 256, 320, banks[0][:, 128:192])
+        product(1, 0, 128, 256, banks[0][:, 0:128])
 
-        y_tap1 = [keep.tile([P, V], F32, name=f"y_tap1{b}") for b in range(2)]
-        y_last = keep.tile([P, PIECE], F32, name="y_last")
-        for i, (c0, c1) in enumerate(cuts):
-            product(1, 0, c0, c1, banks[3 + 3 * i][:, 0:PIECE])
-            nc.scalar.copy(y_tap1[0][:, c0:c1], banks[3 + 3 * i][:, 0:PIECE])
-        scatter(1, 0, 0, V, y_tap1[0][:])
-        product(0, 1, PIECE, V, banks[6][:, 0:PIECE])
-        nc.scalar.copy(y_last[:], banks[6][:, 0:PIECE])
-        scatter(0, 1, PIECE, V, y_last[:])
-        product(1, 1, 0, V, banks[4][:, 0:V])
-        nc.scalar.copy(y_tap1[1][:], banks[4][:, 0:V])
-        scatter(1, 1, 0, V, y_tap1[1][:])
+        scatter_v(0, 0, 192, 256, y_rest[:, 0, 0:64])
+        scatter_s(1, 0, 0, 64, y_rest[:, 1, 0:64])
+        nc.scalar.copy(y_rest[:, 0, :], banks[1][:, 0:192])
+        nc.vector.tensor_copy(y_rest[:, 1, :], banks[0][:, 0:192])
+        product(1, 1, 64, 320, banks[0][:, 0:256])
+        product(0, 1, 320, 448, banks[1][:, 0:128])
+        product(0, 1, 448, 512, banks[1][:, 128:192])
+        product(0, 1, 0, 64, banks[1][:, 192:256])
+        scatter_v(0, 0, 0, 192, y_rest[:, 0, :])
+        scatter_s(1, 0, 64, 256, y_rest[:, 1, :])
+        nc.vector.tensor_copy(y_late[1][:], banks[0][:, 0:256])
+        nc.scalar.copy(y_late[0][:], banks[1][:, 0:256])
+        scatter_s(1, 1, 0, 256, y_late[1][:])
+        scatter_v(0, 1, 0, 256, y_late[0][:])
 
-        sum0 = [keep.tile([P, HALF], F32, name=f"sum0{h}") for h in range(2)]
+        sum0 = [keep.tile([P, HALF], F32, name=f"sum0{h}", tag=f"sums{h}") for h in range(2)]
         result0 = [keep.tile([P, HALF], F32, name=f"result0{h}") for h in range(2)]
         for h in range(2):
             cols = slice(h * HALF, (h + 1) * HALF)
             nc.gpsimd.tensor_tensor(sum0[h][:], spread[0][0][:, cols], spread[1][0][:, cols], ADD)
             nc.scalar.activation(result0[h][:], sum0[h][:], RELU)
-            nc.scalar.dma_start(out[0:P, cols], result0[h][:])
+            nc.sync.dma_start(out[0:P, cols], result0[h][:])
 
         edges = [0, 128, 384, 512]
         shares = [slice(a, b) for a, b in zip(edges[:-1], edges[1:])]
-        total = [keep.tile([P, c.stop - c.start], F32, name=f"total{c.start}") for c in shares]
+        tags = ["total0", "total1", "total2"]
+        total = [keep.tile([P, c.stop - c.start], F32, name=f"total{c.start}", tag=t) for c, t in zip(shares, tags)]
         result1 = [keep.tile([P, c.stop - c.start], F32, name=f"result1{c.start}") for c in shares]
 
         def add(h):

@@ -47,44 +47,45 @@ def tile_picked_spconv_relu_e_kernel(
         def load_words(d, words):
             nc.sync.dma_start(w_codes[d][:].bitcast(I32), words[0].rearrange("p n r -> p (n r)").bitcast(I32))
 
-        def load_scales(engine, d, scales):
-            for q in range(4):
+        def load_scales(engine, d, scales, quadrants):
+            for q in quadrants:
                 engine.dma_start(
                     w_scales[d][32 * q : 32 * q + 4, :].bitcast(I32), scales[0, 4 * q : 4 * q + 4, :].bitcast(I32)
                 )
 
-        load_scales(nc.gpsimd, 1, w2_scales)
+        load_scales(nc.scalar, 0, w1_scales, range(4))
+        load_scales(nc.gpsimd, 1, w2_scales, range(3))
         nc.sync.dma_start(rows[0][:], x_rows[0])
         nc.sync.dma_start(picks[:], offs)
+        for j in range(1, PACK - 1):
+            nc.sync.dma_start(rows[j][:], x_rows[j])
+        load_scales(nc.sync, 1, w2_scales, range(3, 4))
+        nc.sync.dma_start(rows[PACK - 1][:], x_rows[PACK - 1])
+        load_words(0, w1_words)
+        load_words(1, w2_words)
         nc.sync.dma_start(places[0][:], to1)
         nc.sync.dma_start(places[1][:], to2)
-        for j in range(1, PACK):
-            nc.sync.dma_start(rows[j][:], x_rows[j])
-        load_words(1, w2_words)
-        load_words(0, w1_words)
-        load_scales(nc.sync, 0, w1_scales)
 
         for d, b in ((0, 0), (0, 1), (1, 0)):
             nc.vector.memset(spread[d][b][:], 0.0)
         nc.scalar.activation(spread[1][1][:], spread[0][0][:], COPY)
 
-        SHIFT = 192
         x_codes = keep.tile([P, S], U32, name="x_codes", align_bytes=64)
         x_scales = keep.tile([P, S], U8, name="x_scales", align_bytes=64)
 
-        def offsets(c0, c1):
-            e0 = (c0 + SHIFT) % S
-            return picks[:, e0 // GROUP : (e0 + c1 - c0) // GROUP]
+        def offsets(e0, e1):
+            return picks[:, e0 // GROUP : e1 // GROUP]
 
         PIECE = 128
-        woven = [keep.tile([P, PIECE * PACK], BF16, name=f"woven{i}", align_bytes=64) for i in range(4)]
+        woven_mid = keep.tile([P, 2 * PIECE * PACK], BF16, name="woven_mid", align_bytes=64)
+        woven_end = [keep.tile([P, PIECE * PACK], BF16, name=f"woven_end{d}", align_bytes=64) for d in range(2)]
 
-        def lanes(i):
-            return woven[i][:].rearrange("p (c j) -> p c j", j=PACK)
+        def lanes(woven):
+            return woven[:].rearrange("p (c j) -> p c j", j=PACK)
 
-        def quantise(i):
-            cols = slice(i * PIECE, (i + 1) * PIECE)
-            nc.vector.quantize_mx(out=x_codes[:, cols].bitcast(FP8X4), scales=x_scales[:, cols], in_=woven[i][:])
+        def quantise(src, e0):
+            cols = slice(e0, e0 + PIECE)
+            nc.vector.quantize_mx(out=x_codes[:, cols].bitcast(FP8X4), scales=x_scales[:, cols], in_=src)
 
         def product(d, b, c0, c1, acc):
             m_cols = slice(b * P, (b + 1) * P)
@@ -98,37 +99,37 @@ def tile_picked_spconv_relu_e_kernel(
                 stop=True,
             )
 
-        def gather_woven(i, j):
-            nc.vector.tensor_copy(lanes(i)[:, :, j], rows[j][:].indirect(offsets(i * PIECE, (i + 1) * PIECE)))
+        ends = [0, 3 * PIECE]
+        stage = [keep.tile([P, PACK, PIECE], BF16, name=f"stage{d}") for d in range(2)]
 
-        def gather_plain(dst, j, c0, c1):
-            nc.scalar.activation(dst, rows[j][:].indirect(offsets(c0, c1)), COPY)
+        def gather_woven(j, c0, c1):
+            nc.vector.tensor_copy(lanes(woven_mid)[:, c0:c1, j], rows[j][:].indirect(offsets(PIECE + c0, PIECE + c1)))
 
-        low = keep.tile([P, 2, 2 * PIECE], BF16, name="low")
-        high = [None] + [keep.tile([P, 2, PIECE], BF16, name=f"high{i}") for i in range(1, 3)]
+        def gather_staged(j):
+            for d in (1, 0):
+                nc.scalar.activation(stage[d][:, j, :], rows[j][:].indirect(offsets(ends[d], ends[d] + PIECE)), COPY)
 
-        for j in range(2):
-            gather_woven(0, j)
-            gather_woven(3, j)
-            gather_plain(low[:, j, 0:192], j, 128, 320)
-            gather_plain(low[:, j, 192:256], j, 320, 384)
-        for i in range(1, 3):
-            nc.vector.tensor_copy(
-                lanes(i)[:, :, 0:2], low[:, :, (i - 1) * PIECE : i * PIECE].rearrange("p j c -> p c j")
-            )
-        for j in range(2, 4):
-            gather_woven(0, j)
-            gather_woven(3, j)
-            gather_plain(high[1][:, j - 2, :], j, 128, 256)
-            gather_plain(high[2][:, j - 2, 0:64], j, 256, 320)
-            gather_plain(high[2][:, j - 2, 64:128], j, 320, 384)
+        def weave(copy, d, pair):
+            js = slice(2 * pair, 2 * pair + 2)
+            copy(lanes(woven_end[d])[:, :, js], stage[d][:, js, :].rearrange("p j c -> p c j"))
 
-        def weave(engine_copy, i):
-            engine_copy(lanes(i)[:, :, 2:4], high[i][:].rearrange("p j c -> p c j"))
+        for j in range(3):
+            gather_woven(j, 0, 2 * PIECE)
+            gather_staged(j)
+            if j == 1:
+                weave(nc.vector.tensor_copy, 1, 0)
+                weave(nc.scalar.copy, 0, 0)
+        gather_woven(3, 0, PIECE)
+        gather_woven(3, PIECE, 2 * PIECE)
+        gather_staged(3)
+        weave(nc.scalar.copy, 1, 1)
+        weave(nc.scalar.copy, 0, 1)
 
-        banks = [psum.tile([P, U], F32, name=f"bank{i}") for i in range(2)]
-        y_rest = keep.tile([P, 2, 192], F32, name="y_rest")
-        y_late = [keep.tile([P, V], F32, name=f"y_late{d}") for d in range(2)]
+        banks = [psum.tile([P, U], F32, name=f"bank{i}") for i in range(6)]
+        y_tap = [keep.tile([P, PIECE + V], F32, name=f"y_tap{d}") for d in range(2)]
+        y_first = [y[:, PIECE // 2 : PIECE // 2 + PIECE] for y in y_tap]
+        y_rest = [y[:, 0:PIECE] for y in y_tap]
+        y_late = [y[:, PIECE : PIECE + V] for y in y_tap]
 
         def scatter_v(d, b, v0, v1, y):
             nc.vector.tensor_copy(spread[d][b][:].indirect(places[d][:, v0 // GROUP : v1 // GROUP]), y)
@@ -136,34 +137,29 @@ def tile_picked_spconv_relu_e_kernel(
         def scatter_s(d, b, v0, v1, y):
             nc.scalar.activation(spread[d][b][:].indirect(places[d][:, v0 // GROUP : v1 // GROUP]), y, COPY)
 
-        quantise(0)
-        product(1, 0, 64, 128, banks[0][:, 64:128])
-        product(0, 0, 0, 64, banks[0][:, 0:64])
-        weave(nc.scalar.copy, 2)
-        nc.scalar.copy(y_rest[:, :, 0:64], banks[0][:, 0:128].rearrange("p (d c) -> p d c", d=2))
-        quantise(3)
-        product(0, 0, 384, 512, banks[1][:, 64:192])
-        weave(nc.vector.tensor_copy, 1)
-        quantise(2)
-        quantise(1)
-        product(0, 0, 320, 384, banks[1][:, 0:64])
-        product(1, 0, 256, 320, banks[0][:, 128:192])
-        product(1, 0, 128, 256, banks[0][:, 0:128])
+        quantise(woven_mid[:, 0 : PIECE * PACK], 128)
+        product(0, 0, 128, 256, banks[0][:, 0:128])
+        nc.scalar.copy(y_first[0], banks[0][:, 0:128])
+        quantise(woven_mid[:, PIECE * PACK : 2 * PIECE * PACK], 256)
+        product(1, 0, 256, 384, banks[1][:, 0:128])
+        nc.scalar.copy(y_first[1], banks[1][:, 0:128])
+        quantise(woven_end[1][:], 384)
+        product(1, 0, 384, 512, banks[2][:, 0:128])
+        product(1, 1, 256, 512, banks[3][:, 0:256])
+        quantise(woven_end[0][:], 0)
+        product(0, 0, 0, 128, banks[4][:, 0:128])
+        product(0, 1, 0, 256, banks[5][:, 0:256])
 
-        scatter_v(0, 0, 192, 256, y_rest[:, 0, 0:64])
-        scatter_s(1, 0, 0, 64, y_rest[:, 1, 0:64])
-        nc.scalar.copy(y_rest[:, 0, :], banks[1][:, 0:192])
-        nc.vector.tensor_copy(y_rest[:, 1, :], banks[0][:, 0:192])
-        product(1, 1, 64, 320, banks[0][:, 0:256])
-        product(0, 1, 320, 448, banks[1][:, 0:128])
-        product(0, 1, 448, 512, banks[1][:, 128:192])
-        product(0, 1, 0, 64, banks[1][:, 192:256])
-        scatter_v(0, 0, 0, 192, y_rest[:, 0, :])
-        scatter_s(1, 0, 64, 256, y_rest[:, 1, :])
-        nc.vector.tensor_copy(y_late[1][:], banks[0][:, 0:256])
-        nc.scalar.copy(y_late[0][:], banks[1][:, 0:256])
-        scatter_s(1, 1, 0, 256, y_late[1][:])
-        scatter_v(0, 1, 0, 256, y_late[0][:])
+        scatter_v(0, 0, 128, 256, y_first[0])
+        scatter_s(1, 0, 0, 128, y_first[1])
+        nc.scalar.copy(y_rest[1], banks[2][:, 0:128])
+        nc.scalar.copy(y_late[1], banks[3][:, 0:256])
+        nc.vector.tensor_copy(y_rest[0], banks[4][:, 0:128])
+        nc.vector.tensor_copy(y_late[0], banks[5][:, 0:256])
+        scatter_v(0, 0, 0, 128, y_rest[0])
+        scatter_s(1, 0, 128, 256, y_rest[1])
+        scatter_v(0, 1, 0, 256, y_late[0])
+        scatter_s(1, 1, 0, 256, y_late[1])
 
         sum0 = [keep.tile([P, HALF], F32, name=f"sum0{h}", tag=f"sums{h}") for h in range(2)]
         result0 = [keep.tile([P, HALF], F32, name=f"result0{h}") for h in range(2)]

@@ -123,7 +123,6 @@ def tile_picked_spconv_relu_e_kernel(
         gather_woven(3, PIECE, 2 * PIECE)
         gather_staged(3)
         weave(nc.scalar.copy, 1, 1)
-        weave(nc.scalar.copy, 0, 1)
 
         banks = [psum.tile([P, U], F32, name=f"bank{i}") for i in range(6)]
         y_tap = [keep.tile([P, PIECE + V], F32, name=f"y_tap{d}") for d in range(2)]
@@ -143,6 +142,7 @@ def tile_picked_spconv_relu_e_kernel(
         quantise(woven_mid[:, PIECE * PACK : 2 * PIECE * PACK], 256)
         product(1, 0, 256, 384, banks[1][:, 0:128])
         nc.scalar.copy(y_first[1], banks[1][:, 0:128])
+        weave(nc.vector.tensor_copy, 0, 1)
         quantise(woven_end[1][:], 384)
         product(1, 0, 384, 512, banks[2][:, 0:128])
         product(1, 1, 256, 512, banks[3][:, 0:256])
@@ -161,26 +161,28 @@ def tile_picked_spconv_relu_e_kernel(
         scatter_v(0, 1, 0, 256, y_late[0])
         scatter_s(1, 1, 0, 256, y_late[1])
 
-        sum0 = [keep.tile([P, HALF], F32, name=f"sum0{h}", tag=f"sums{h}") for h in range(2)]
+        sum_low = keep.tile([P, HALF], F32, name="sum_low", tag="sums")
         result0 = [keep.tile([P, HALF], F32, name=f"result0{h}") for h in range(2)]
-        for h in range(2):
-            cols = slice(h * HALF, (h + 1) * HALF)
-            nc.gpsimd.tensor_tensor(sum0[h][:], spread[0][0][:, cols], spread[1][0][:, cols], ADD)
-            nc.scalar.activation(result0[h][:], sum0[h][:], RELU)
-            nc.sync.dma_start(out[0:P, cols], result0[h][:])
+        low, high = slice(0, HALF), slice(HALF, U)
+        nc.gpsimd.tensor_tensor(sum_low[:], spread[0][0][:, low], spread[1][0][:, low], ADD)
+        nc.vector.tensor_scalar_max(result0[0][:], sum_low[:], 0.0)
+        nc.sync.dma_start(out[0:P, low], result0[0][:])
+        sum_high = spread[0][0][:, low]
+        nc.vector.tensor_tensor(sum_high, spread[0][0][:, high], spread[1][0][:, high], ADD)
+        nc.scalar.activation(result0[1][:], sum_high, RELU)
+        nc.sync.dma_start(out[0:P, high], result0[1][:])
 
-        edges = [0, 128, 384, 512]
+        edges = [0, 192, 384, 512]
         shares = [slice(a, b) for a, b in zip(edges[:-1], edges[1:])]
-        tags = ["total0", "total1", "total2"]
-        total = [keep.tile([P, c.stop - c.start], F32, name=f"total{c.start}", tag=t) for c, t in zip(shares, tags)]
+        total_first = keep.tile([P, edges[1]], F32, name="total_first", tag="sums")
+        total = [total_first[:], spread[1][0][:, 0:192], spread[1][0][:, edges[2] : U]]
         result1 = [keep.tile([P, c.stop - c.start], F32, name=f"result1{c.start}") for c in shares]
 
-        def add(h):
-            nc.vector.tensor_tensor(total[h][:], spread[0][1][:, shares[h]], spread[1][1][:, shares[h]], ADD)
-
-        add(0)
         for h, cols in enumerate(shares):
-            if h + 1 < len(shares):
-                add(h + 1)
-            nc.vector.tensor_scalar_max(result1[h][:], total[h][:], 0.0)
+            nc.vector.tensor_tensor(total[h], spread[0][1][:, cols], spread[1][1][:, cols], ADD)
+        for h, cols in enumerate(shares):
+            if h == 0:
+                nc.scalar.activation(result1[h][:], total[h], RELU)
+            else:
+                nc.vector.tensor_scalar_max(result1[h][:], total[h], 0.0)
             nc.sync.dma_start(out[P : 2 * P, cols], result1[h][:])

@@ -54,12 +54,11 @@ def tile_picked_spconv_relu_e_kernel(
                 )
 
         load_scales(nc.scalar, 0, w1_scales, range(4))
-        load_scales(nc.gpsimd, 1, w2_scales, range(3))
+        load_scales(nc.gpsimd, 1, w2_scales, range(4))
         nc.sync.dma_start(rows[0][:], x_rows[0])
         nc.sync.dma_start(picks[:], offs)
         for j in range(1, PACK - 1):
             nc.sync.dma_start(rows[j][:], x_rows[j])
-        load_scales(nc.sync, 1, w2_scales, range(3, 4))
         nc.sync.dma_start(rows[PACK - 1][:], x_rows[PACK - 1])
         load_words(0, w1_words)
         load_words(1, w2_words)
@@ -124,7 +123,7 @@ def tile_picked_spconv_relu_e_kernel(
         gather_staged(3)
         weave(nc.scalar.copy, 1, 1)
 
-        banks = [psum.tile([P, U], F32, name=f"bank{i}") for i in range(6)]
+        banks = [psum.tile([P, U], F32, name=f"bank{i}") for i in range(4)]
         y_tap = [keep.tile([P, PIECE + V], F32, name=f"y_tap{d}") for d in range(2)]
         y_first = [y[:, PIECE // 2 : PIECE // 2 + PIECE] for y in y_tap]
         y_rest = [y[:, 0:PIECE] for y in y_tap]
@@ -147,15 +146,15 @@ def tile_picked_spconv_relu_e_kernel(
         product(1, 0, 384, 512, banks[2][:, 0:128])
         product(1, 1, 256, 512, banks[3][:, 0:256])
         quantise(woven_end[0][:], 0)
-        product(0, 0, 0, 128, banks[4][:, 0:128])
-        product(0, 1, 0, 256, banks[5][:, 0:256])
+        product(0, 0, 0, 128, banks[1][:, 128:256])
+        product(0, 1, 0, 256, banks[1][:, 256:512])
 
         scatter_v(0, 0, 128, 256, y_first[0])
         scatter_s(1, 0, 0, 128, y_first[1])
         nc.scalar.copy(y_rest[1], banks[2][:, 0:128])
         nc.scalar.copy(y_late[1], banks[3][:, 0:256])
-        nc.vector.tensor_copy(y_rest[0], banks[4][:, 0:128])
-        nc.vector.tensor_copy(y_late[0], banks[5][:, 0:256])
+        nc.vector.tensor_copy(y_rest[0], banks[1][:, 128:256])
+        nc.vector.tensor_copy(y_late[0], banks[1][:, 256:512])
         scatter_v(0, 0, 0, 128, y_rest[0])
         scatter_s(1, 0, 128, 256, y_rest[1])
         scatter_v(0, 1, 0, 256, y_late[0])

@@ -54,13 +54,14 @@ def tile_picked_spconv_relu_e_kernel(
                 )
 
         load_scales(nc.scalar, 0, w1_scales, range(4))
-        load_scales(nc.gpsimd, 1, w2_scales, range(4))
         nc.sync.dma_start(rows[0][:], x_rows[0])
         nc.sync.dma_start(picks[:], offs)
         for j in range(1, PACK - 1):
             nc.sync.dma_start(rows[j][:], x_rows[j])
+        load_scales(nc.sync, 1, w2_scales, range(1))
         nc.sync.dma_start(rows[PACK - 1][:], x_rows[PACK - 1])
         load_words(0, w1_words)
+        load_scales(nc.sync, 1, w2_scales, range(1, 4))
         load_words(1, w2_words)
         nc.sync.dma_start(places[0][:], to1)
         nc.sync.dma_start(places[1][:], to2)

@@ -36,11 +36,10 @@ def tile_picked_spconv_relu_e_kernel(
         places = [keep.tile([P, V // GROUP], U16, name=f"places{d}") for d in range(2)]
         rows = [keep.tile([P, T], F32, name=f"rows{j}") for j in range(PACK)]
         w_codes = [keep.tile([P, N], U32, name=f"w_codes{d}", align_bytes=64) for d in range(2)]
-        w_scales = [keep.tile([P, N], U8, name=f"w_scales{d}", align_bytes=64) for d in range(2)]
+        w_scales = keep.tile([P, N], U8, name="w_scales", align_bytes=64)
         spread = [[keep.tile([P, U], F32, name=f"spread{d}{b}") for b in range(2)] for d in range(2)]
 
-        for d in range(2):
-            nc.gpsimd.memset(w_scales[d][:].bitcast(I32), 0)
+        nc.gpsimd.memset(w_scales[:].bitcast(I32), 0)
 
         x_rows = xT.rearrange("(p j) t -> j p t", j=PACK)
 
@@ -50,19 +49,17 @@ def tile_picked_spconv_relu_e_kernel(
         def load_scales(engine, d, scales, quadrants):
             for q in quadrants:
                 engine.dma_start(
-                    w_scales[d][32 * q : 32 * q + 4, :].bitcast(I32), scales[0, 4 * q : 4 * q + 4, :].bitcast(I32)
+                    w_scales[32 * q + 4 * d : 32 * q + 4 * d + 4, :].bitcast(I32), scales[0, 4 * q : 4 * q + 4, :].bitcast(I32)
                 )
 
         load_scales(nc.scalar, 0, w1_scales, range(4))
         nc.sync.dma_start(rows[0][:], x_rows[0])
         nc.sync.dma_start(picks[:], offs)
-        for j in range(1, PACK - 1):
+        for j in range(1, PACK):
             nc.sync.dma_start(rows[j][:], x_rows[j])
-        load_scales(nc.sync, 1, w2_scales, range(1))
-        nc.sync.dma_start(rows[PACK - 1][:], x_rows[PACK - 1])
         load_words(0, w1_words)
-        load_scales(nc.sync, 1, w2_scales, range(1, 4))
         load_words(1, w2_words)
+        load_scales(nc.sync, 1, w2_scales, range(4))
         nc.sync.dma_start(places[0][:], to1)
         nc.sync.dma_start(places[1][:], to2)
 
@@ -92,7 +89,7 @@ def tile_picked_spconv_relu_e_kernel(
             nc.tensor.matmul_mx(
                 out=acc,
                 lhsT=w_codes[d][:, m_cols].bitcast(FP8X4),
-                lhsT_scale=w_scales[d][:, m_cols],
+                lhsT_scale=w_scales[4 * d : P, m_cols],
                 rhs=x_codes[:, c0:c1].bitcast(FP8X4),
                 rhs_scale=x_scales[:, c0:c1],
                 start=True,
@@ -123,8 +120,9 @@ def tile_picked_spconv_relu_e_kernel(
         gather_woven(3, PIECE, 2 * PIECE)
         gather_staged(3)
         weave(nc.scalar.copy, 1, 1)
+        weave(nc.scalar.copy, 0, 1)
 
-        banks = [psum.tile([P, U], F32, name=f"bank{i}") for i in range(4)]
+        banks = [psum.tile([P, U], F32, name=f"bank{i}") for i in range(6)]
         y_tap = [keep.tile([P, PIECE + V], F32, name=f"y_tap{d}") for d in range(2)]
         y_first = [y[:, PIECE // 2 : PIECE // 2 + PIECE] for y in y_tap]
         y_rest = [y[:, 0:PIECE] for y in y_tap]
@@ -142,20 +140,19 @@ def tile_picked_spconv_relu_e_kernel(
         quantise(woven_mid[:, PIECE * PACK : 2 * PIECE * PACK], 256)
         product(1, 0, 256, 384, banks[1][:, 0:128])
         nc.scalar.copy(y_first[1], banks[1][:, 0:128])
-        weave(nc.vector.tensor_copy, 0, 1)
         quantise(woven_end[1][:], 384)
         product(1, 0, 384, 512, banks[2][:, 0:128])
         product(1, 1, 256, 512, banks[3][:, 0:256])
         quantise(woven_end[0][:], 0)
-        product(0, 0, 0, 128, banks[1][:, 128:256])
-        product(0, 1, 0, 256, banks[1][:, 256:512])
+        product(0, 0, 0, 128, banks[4][:, 0:128])
+        product(0, 1, 0, 256, banks[5][:, 0:256])
 
         scatter_v(0, 0, 128, 256, y_first[0])
         scatter_s(1, 0, 0, 128, y_first[1])
         nc.scalar.copy(y_rest[1], banks[2][:, 0:128])
         nc.scalar.copy(y_late[1], banks[3][:, 0:256])
-        nc.vector.tensor_copy(y_rest[0], banks[1][:, 128:256])
-        nc.vector.tensor_copy(y_late[0], banks[1][:, 256:512])
+        nc.vector.tensor_copy(y_rest[0], banks[4][:, 0:128])
+        nc.vector.tensor_copy(y_late[0], banks[5][:, 0:256])
         scatter_v(0, 0, 0, 128, y_rest[0])
         scatter_s(1, 0, 128, 256, y_rest[1])
         scatter_v(0, 1, 0, 256, y_late[0])

@@ -53,14 +53,14 @@ def tile_picked_spconv_relu_e_kernel(
                 )
 
         load_scales(nc.scalar, 0, w1_scales, range(4))
-        nc.sync.dma_start(rows[0][:], x_rows[0])
+        load_scales(nc.scalar, 1, w2_scales, range(1))
         nc.sync.dma_start(picks[:], offs)
-        for j in range(1, PACK):
+        for j in range(PACK):
             nc.sync.dma_start(rows[j][:], x_rows[j])
+        nc.sync.dma_start(places[0][:], to1)
         load_words(0, w1_words)
         load_words(1, w2_words)
-        load_scales(nc.sync, 1, w2_scales, range(4))
-        nc.sync.dma_start(places[0][:], to1)
+        load_scales(nc.sync, 1, w2_scales, range(1, 4))
         nc.sync.dma_start(places[1][:], to2)
 
         for d, b in ((0, 0), (0, 1), (1, 0)):
@@ -116,15 +116,16 @@ def tile_picked_spconv_relu_e_kernel(
             if j == 1:
                 weave(nc.vector.tensor_copy, 1, 0)
                 weave(nc.scalar.copy, 0, 0)
-        gather_woven(3, 0, PIECE)
         gather_woven(3, PIECE, 2 * PIECE)
+        gather_woven(3, 0, PIECE)
         gather_staged(3)
         weave(nc.scalar.copy, 1, 1)
         weave(nc.scalar.copy, 0, 1)
 
-        banks = [psum.tile([P, U], F32, name=f"bank{i}") for i in range(6)]
+        banks = [psum.tile([P, U], F32, name=f"bank{i}") for i in range(4)]
         y_tap = [keep.tile([P, PIECE + V], F32, name=f"y_tap{d}") for d in range(2)]
-        y_first = [y[:, PIECE // 2 : PIECE // 2 + PIECE] for y in y_tap]
+        y_first0 = keep.tile([P, PIECE], F32, name="y_first0")
+        y_first = [y_first0[:], y_tap[1][:, PIECE // 2 : PIECE // 2 + PIECE]]
         y_rest = [y[:, 0:PIECE] for y in y_tap]
         y_late = [y[:, PIECE : PIECE + V] for y in y_tap]
 
@@ -134,25 +135,25 @@ def tile_picked_spconv_relu_e_kernel(
         def scatter_s(d, b, v0, v1, y):
             nc.scalar.activation(spread[d][b][:].indirect(places[d][:, v0 // GROUP : v1 // GROUP]), y, COPY)
 
-        quantise(woven_mid[:, 0 : PIECE * PACK], 128)
-        product(0, 0, 128, 256, banks[0][:, 0:128])
-        nc.scalar.copy(y_first[0], banks[0][:, 0:128])
         quantise(woven_mid[:, PIECE * PACK : 2 * PIECE * PACK], 256)
         product(1, 0, 256, 384, banks[1][:, 0:128])
         nc.scalar.copy(y_first[1], banks[1][:, 0:128])
+        quantise(woven_mid[:, 0 : PIECE * PACK], 128)
+        product(0, 0, 128, 256, banks[0][:, 0:128])
+        nc.scalar.copy(y_first[0], banks[0][:, 0:128])
         quantise(woven_end[1][:], 384)
         product(1, 0, 384, 512, banks[2][:, 0:128])
         product(1, 1, 256, 512, banks[3][:, 0:256])
         quantise(woven_end[0][:], 0)
-        product(0, 0, 0, 128, banks[4][:, 0:128])
-        product(0, 1, 0, 256, banks[5][:, 0:256])
+        product(0, 0, 0, 128, banks[0][:, 128:256])
+        product(0, 1, 0, 256, banks[0][:, 256:512])
 
         scatter_v(0, 0, 128, 256, y_first[0])
         scatter_s(1, 0, 0, 128, y_first[1])
         nc.scalar.copy(y_rest[1], banks[2][:, 0:128])
         nc.scalar.copy(y_late[1], banks[3][:, 0:256])
-        nc.vector.tensor_copy(y_rest[0], banks[4][:, 0:128])
-        nc.vector.tensor_copy(y_late[0], banks[5][:, 0:256])
+        nc.vector.tensor_copy(y_rest[0], banks[0][:, 128:256])
+        nc.vector.tensor_copy(y_late[0], banks[0][:, 256:512])
         scatter_v(0, 0, 0, 128, y_rest[0])
         scatter_s(1, 0, 128, 256, y_rest[1])
         scatter_v(0, 1, 0, 256, y_late[0])
@@ -162,17 +163,16 @@ def tile_picked_spconv_relu_e_kernel(
         result0 = [keep.tile([P, HALF], F32, name=f"result0{h}") for h in range(2)]
         low, high = slice(0, HALF), slice(HALF, U)
         nc.gpsimd.tensor_tensor(sum_low[:], spread[0][0][:, low], spread[1][0][:, low], ADD)
-        nc.vector.tensor_scalar_max(result0[0][:], sum_low[:], 0.0)
+        nc.scalar.activation(result0[0][:], sum_low[:], RELU)
         nc.sync.dma_start(out[0:P, low], result0[0][:])
         sum_high = spread[0][0][:, low]
-        nc.vector.tensor_tensor(sum_high, spread[0][0][:, high], spread[1][0][:, high], ADD)
+        nc.gpsimd.tensor_tensor(sum_high, spread[0][0][:, high], spread[1][0][:, high], ADD)
         nc.scalar.activation(result0[1][:], sum_high, RELU)
         nc.sync.dma_start(out[0:P, high], result0[1][:])
 
         edges = [0, 192, 384, 512]
         shares = [slice(a, b) for a, b in zip(edges[:-1], edges[1:])]
-        total_first = keep.tile([P, edges[1]], F32, name="total_first", tag="sums")
-        total = [total_first[:], spread[1][0][:, 0:192], spread[1][0][:, edges[2] : U]]
+        total = [spread[1][0][:, 0:192], spread[1][0][:, 192:384], spread[1][0][:, edges[2] : U]]
         result1 = [keep.tile([P, c.stop - c.start], F32, name=f"result1{c.start}") for c in shares]
 
         for h, cols in enumerate(shares):

@@ -122,7 +122,7 @@ def tile_picked_spconv_relu_e_kernel(
         weave(nc.scalar.copy, 1, 1)
         weave(nc.scalar.copy, 0, 1)
 
-        banks = [psum.tile([P, U], F32, name=f"bank{i}") for i in range(4)]
+        banks = [psum.tile([P, U], F32, name=f"bank{i}") for i in range(5)]
         y_tap = [keep.tile([P, PIECE + V], F32, name=f"y_tap{d}") for d in range(2)]
         y_first0 = keep.tile([P, PIECE], F32, name="y_first0")
         y_first = [y_first0[:], y_tap[1][:, PIECE // 2 : PIECE // 2 + PIECE]]
@@ -141,19 +141,22 @@ def tile_picked_spconv_relu_e_kernel(
         quantise(woven_mid[:, 0 : PIECE * PACK], 128)
         product(0, 0, 128, 256, banks[0][:, 0:128])
         nc.scalar.copy(y_first[0], banks[0][:, 0:128])
+        product(0, 1, 128, 256, banks[4][:, 0:128])
+        nc.vector.tensor_copy(y_late[0][:, 128:256], banks[4][:, 0:128])
+        product(1, 1, 256, 384, banks[3][:, 0:128])
         quantise(woven_end[1][:], 384)
         product(1, 0, 384, 512, banks[2][:, 0:128])
-        product(1, 1, 256, 512, banks[3][:, 0:256])
+        product(1, 1, 384, 512, banks[3][:, 128:256])
         quantise(woven_end[0][:], 0)
         product(0, 0, 0, 128, banks[0][:, 128:256])
-        product(0, 1, 0, 256, banks[0][:, 256:512])
+        product(0, 1, 0, 128, banks[0][:, 256:384])
 
         scatter_v(0, 0, 128, 256, y_first[0])
         scatter_s(1, 0, 0, 128, y_first[1])
         nc.scalar.copy(y_rest[1], banks[2][:, 0:128])
         nc.scalar.copy(y_late[1], banks[3][:, 0:256])
         nc.vector.tensor_copy(y_rest[0], banks[0][:, 128:256])
-        nc.vector.tensor_copy(y_late[0], banks[0][:, 256:512])
+        nc.vector.tensor_copy(y_late[0][:, 0:128], banks[0][:, 256:384])
         scatter_v(0, 0, 0, 128, y_rest[0])
         scatter_s(1, 0, 128, 256, y_rest[1])
         scatter_v(0, 1, 0, 256, y_late[0])

@@ -15,13 +15,17 @@ FP8X4 = mybir.dt.float8_e4m3fn_x4
 COPY = mybir.ActivationFunctionType.Copy
 RELU = mybir.ActivationFunctionType.Relu
 ADD = mybir.AluOpType.add
-MULT = mybir.AluOpType.mult
-MAX = mybir.AluOpType.max
 
 P = 128
 PACK = 4
 GROUP = 16
+QUADRANT = 32
+SCALE_ROWS = 4
+PIECE = V // 2
 HALF = U // 2
+INNER = (PIECE, V)
+OUTER = (0, V + PIECE)
+EDGES = (0, 192, 384, U)
 
 
 def tile_picked_spconv_relu_e_kernel(
@@ -34,29 +38,30 @@ def tile_picked_spconv_relu_e_kernel(
 
         picks = keep.tile([P, S // GROUP], U16, name="picks")
         places = [keep.tile([P, V // GROUP], U16, name=f"places{d}") for d in range(2)]
-        rows = [keep.tile([P, T], F32, name=f"rows{j}") for j in range(PACK)]
+        planes = [keep.tile([P, T], F32, name=f"plane{j}") for j in range(PACK)]
         w_codes = [keep.tile([P, N], U32, name=f"w_codes{d}", align_bytes=64) for d in range(2)]
         w_scales = keep.tile([P, N], U8, name="w_scales", align_bytes=64)
-        spread = [[keep.tile([P, U], F32, name=f"spread{d}{b}") for b in range(2)] for d in range(2)]
+        windows = [[keep.tile([P, U], F32, name=f"window{d}{b}") for b in range(2)] for d in range(2)]
 
         nc.gpsimd.memset(w_scales[:].bitcast(I32), 0)
-
-        x_rows = xT.rearrange("(p j) t -> j p t", j=PACK)
 
         def load_words(d, words):
             nc.sync.dma_start(w_codes[d][:].bitcast(I32), words[0].rearrange("p n r -> p (n r)").bitcast(I32))
 
         def load_scales(engine, d, scales, quadrants):
             for q in quadrants:
+                first = QUADRANT * q + SCALE_ROWS * d
                 engine.dma_start(
-                    w_scales[32 * q + 4 * d : 32 * q + 4 * d + 4, :].bitcast(I32), scales[0, 4 * q : 4 * q + 4, :].bitcast(I32)
+                    w_scales[first : first + SCALE_ROWS, :].bitcast(I32),
+                    scales[0, SCALE_ROWS * q : SCALE_ROWS * (q + 1), :].bitcast(I32),
                 )
 
         load_scales(nc.scalar, 0, w1_scales, range(4))
         load_scales(nc.scalar, 1, w2_scales, range(1))
         nc.sync.dma_start(picks[:], offs)
+        x_planes = xT.rearrange("(p j) t -> j p t", j=PACK)
         for j in range(PACK):
-            nc.sync.dma_start(rows[j][:], x_rows[j])
+            nc.sync.dma_start(planes[j][:], x_planes[j])
         nc.sync.dma_start(places[0][:], to1)
         load_words(0, w1_words)
         load_words(1, w2_words)
@@ -64,125 +69,126 @@ def tile_picked_spconv_relu_e_kernel(
         nc.sync.dma_start(places[1][:], to2)
 
         for d, b in ((0, 0), (0, 1), (1, 0)):
-            nc.vector.memset(spread[d][b][:], 0.0)
-        nc.scalar.activation(spread[1][1][:], spread[0][0][:], COPY)
+            nc.vector.memset(windows[d][b][:], 0.0)
+        nc.scalar.activation(windows[1][1][:], windows[0][0][:], COPY)
 
         x_codes = keep.tile([P, S], U32, name="x_codes", align_bytes=64)
         x_scales = keep.tile([P, S], U8, name="x_scales", align_bytes=64)
+        woven_inner = keep.tile([P, 2 * PIECE * PACK], BF16, name="woven_inner", align_bytes=64)
+        woven_outer = [keep.tile([P, PIECE * PACK], BF16, name=f"woven_outer{d}", align_bytes=64) for d in range(2)]
+        staged = [keep.tile([P, PACK, PIECE], BF16, name=f"staged{d}") for d in range(2)]
 
-        def offsets(e0, e1):
-            return picks[:, e0 // GROUP : e1 // GROUP]
-
-        PIECE = 128
-        woven_mid = keep.tile([P, 2 * PIECE * PACK], BF16, name="woven_mid", align_bytes=64)
-        woven_end = [keep.tile([P, PIECE * PACK], BF16, name=f"woven_end{d}", align_bytes=64) for d in range(2)]
-
-        def lanes(woven):
+        def by_voxel(woven):
             return woven[:].rearrange("p (c j) -> p c j", j=PACK)
 
-        def quantise(src, e0):
-            cols = slice(e0, e0 + PIECE)
-            nc.vector.quantize_mx(out=x_codes[:, cols].bitcast(FP8X4), scales=x_scales[:, cols], in_=src)
+        def picked(j, first, count):
+            return planes[j][:].indirect(picks[:, first // GROUP : (first + count) // GROUP])
 
-        def product(d, b, c0, c1, acc):
+        def gather_inner(j, first, count):
+            c0 = first - INNER[0]
+            nc.vector.tensor_copy(by_voxel(woven_inner)[:, c0 : c0 + count, j], picked(j, first, count))
+
+        def gather_outer(j):
+            for d in (1, 0):
+                nc.scalar.activation(staged[d][:, j, :], picked(j, OUTER[d], PIECE), COPY)
+
+        def weave(copy, d, pair):
+            js = slice(2 * pair, 2 * pair + 2)
+            copy(by_voxel(woven_outer[d])[:, :, js], staged[d][:, js, :].rearrange("p j c -> p c j"))
+
+        last = PACK - 1
+        for j in range(last):
+            gather_inner(j, INNER[0], 2 * PIECE)
+            gather_outer(j)
+            if j == 1:
+                weave(nc.vector.tensor_copy, 1, 0)
+                weave(nc.scalar.copy, 0, 0)
+        for d in (1, 0):
+            gather_inner(last, INNER[d], PIECE)
+        gather_outer(last)
+        for d in (1, 0):
+            weave(nc.scalar.copy, d, 1)
+
+        def quantise(woven, first):
+            cols = slice(first, first + PIECE)
+            nc.vector.quantize_mx(out=x_codes[:, cols].bitcast(FP8X4), scales=x_scales[:, cols], in_=woven)
+
+        def product(d, b, first, acc):
             m_cols = slice(b * P, (b + 1) * P)
+            cols = slice(first, first + PIECE)
             nc.tensor.matmul_mx(
                 out=acc,
                 lhsT=w_codes[d][:, m_cols].bitcast(FP8X4),
-                lhsT_scale=w_scales[4 * d : P, m_cols],
-                rhs=x_codes[:, c0:c1].bitcast(FP8X4),
-                rhs_scale=x_scales[:, c0:c1],
+                lhsT_scale=w_scales[SCALE_ROWS * d : P, m_cols],
+                rhs=x_codes[:, cols].bitcast(FP8X4),
+                rhs_scale=x_scales[:, cols],
                 start=True,
                 stop=True,
             )
 
-        ends = [0, 3 * PIECE]
-        stage = [keep.tile([P, PACK, PIECE], BF16, name=f"stage{d}") for d in range(2)]
+        def scatter(d, b, first, count, y):
+            target = windows[d][b][:].indirect(places[d][:, first // GROUP : (first + count) // GROUP])
+            if d == 0:
+                nc.vector.tensor_copy(target, y)
+            else:
+                nc.scalar.activation(target, y, COPY)
 
-        def gather_woven(j, c0, c1):
-            nc.vector.tensor_copy(lanes(woven_mid)[:, c0:c1, j], rows[j][:].indirect(offsets(PIECE + c0, PIECE + c1)))
+        tap_banks = [psum.tile([P, U], F32, name=f"tap_bank{d}") for d in range(2)]
+        inner1_banks = [psum.tile([P, U], F32, name=f"inner1_bank{d}") for d in range(2)]
+        slots = [slice(i * PIECE, (i + 1) * PIECE) for i in range(3)]
+        own_copy = (nc.vector.tensor_copy, nc.scalar.copy)
+        y_outer0 = [keep.tile([P, PIECE], F32, name=f"y_outer0_{d}") for d in range(2)]
+        y_block1 = [keep.tile([P, V], F32, name=f"y_block1_{d}") for d in range(2)]
+        y_inner0 = [keep.tile([P, PIECE], F32, name=f"y_inner0_{d}") for d in range(2)]
 
-        def gather_staged(j):
-            for d in (1, 0):
-                nc.scalar.activation(stage[d][:, j, :], rows[j][:].indirect(offsets(ends[d], ends[d] + PIECE)), COPY)
+        def in_tap(d, first):
+            return slice(first - d * V, first - d * V + PIECE)
 
-        def weave(copy, d, pair):
-            js = slice(2 * pair, 2 * pair + 2)
-            copy(lanes(woven_end[d])[:, :, js], stage[d][:, js, :].rearrange("p j c -> p c j"))
+        for d in (1, 0):
+            c0 = (INNER[d] - INNER[0]) * PACK
+            quantise(woven_inner[:, c0 : c0 + PIECE * PACK], INNER[d])
+            product(d, 0, INNER[d], tap_banks[d][:, slots[0]])
+            nc.scalar.copy(y_inner0[d][:], tap_banks[d][:, slots[0]])
+        for d in range(2):
+            product(d, 1, INNER[d], inner1_banks[d][:, slots[0]])
+            own_copy[d](y_block1[d][:, in_tap(d, INNER[d])], inner1_banks[d][:, slots[0]])
+        for d in (1, 0):
+            quantise(woven_outer[d][:], OUTER[d])
+            for b in range(2):
+                product(d, b, OUTER[d], tap_banks[d][:, slots[1 + b]])
 
-        for j in range(3):
-            gather_woven(j, 0, 2 * PIECE)
-            gather_staged(j)
-            if j == 1:
-                weave(nc.vector.tensor_copy, 1, 0)
-                weave(nc.scalar.copy, 0, 0)
-        gather_woven(3, PIECE, 2 * PIECE)
-        gather_woven(3, 0, PIECE)
-        gather_staged(3)
-        weave(nc.scalar.copy, 1, 1)
-        weave(nc.scalar.copy, 0, 1)
+        for d in range(2):
+            scatter(d, 0, INNER[d] - d * V, PIECE, y_inner0[d][:])
+        for d in (1, 0):
+            own_copy[d](y_outer0[d][:], tap_banks[d][:, slots[1]])
+            own_copy[d](y_block1[d][:, in_tap(d, OUTER[d])], tap_banks[d][:, slots[2]])
+        for d in range(2):
+            scatter(d, 0, OUTER[d] - d * V, PIECE, y_outer0[d][:])
+        for d in range(2):
+            scatter(d, 1, 0, V, y_block1[d][:])
 
-        banks = [psum.tile([P, U], F32, name=f"bank{i}") for i in range(5)]
-        y_tap = [keep.tile([P, PIECE + V], F32, name=f"y_tap{d}") for d in range(2)]
-        y_first0 = keep.tile([P, PIECE], F32, name="y_first0")
-        y_first = [y_first0[:], y_tap[1][:, PIECE // 2 : PIECE // 2 + PIECE]]
-        y_rest = [y[:, 0:PIECE] for y in y_tap]
-        y_late = [y[:, PIECE : PIECE + V] for y in y_tap]
-
-        def scatter_v(d, b, v0, v1, y):
-            nc.vector.tensor_copy(spread[d][b][:].indirect(places[d][:, v0 // GROUP : v1 // GROUP]), y)
-
-        def scatter_s(d, b, v0, v1, y):
-            nc.scalar.activation(spread[d][b][:].indirect(places[d][:, v0 // GROUP : v1 // GROUP]), y, COPY)
-
-        quantise(woven_mid[:, PIECE * PACK : 2 * PIECE * PACK], 256)
-        product(1, 0, 256, 384, banks[1][:, 0:128])
-        nc.scalar.copy(y_first[1], banks[1][:, 0:128])
-        quantise(woven_mid[:, 0 : PIECE * PACK], 128)
-        product(0, 0, 128, 256, banks[0][:, 0:128])
-        nc.scalar.copy(y_first[0], banks[0][:, 0:128])
-        product(0, 1, 128, 256, banks[4][:, 0:128])
-        nc.vector.tensor_copy(y_late[0][:, 128:256], banks[4][:, 0:128])
-        product(1, 1, 256, 384, banks[3][:, 0:128])
-        quantise(woven_end[1][:], 384)
-        product(1, 0, 384, 512, banks[2][:, 0:128])
-        product(1, 1, 384, 512, banks[3][:, 128:256])
-        quantise(woven_end[0][:], 0)
-        product(0, 0, 0, 128, banks[0][:, 128:256])
-        product(0, 1, 0, 128, banks[0][:, 256:384])
-
-        scatter_v(0, 0, 128, 256, y_first[0])
-        scatter_s(1, 0, 0, 128, y_first[1])
-        nc.scalar.copy(y_rest[1], banks[2][:, 0:128])
-        nc.scalar.copy(y_late[1], banks[3][:, 0:256])
-        nc.vector.tensor_copy(y_rest[0], banks[0][:, 128:256])
-        nc.vector.tensor_copy(y_late[0][:, 0:128], banks[0][:, 256:384])
-        scatter_v(0, 0, 0, 128, y_rest[0])
-        scatter_s(1, 0, 128, 256, y_rest[1])
-        scatter_v(0, 1, 0, 256, y_late[0])
-        scatter_s(1, 1, 0, 256, y_late[1])
-
-        sum_low = keep.tile([P, HALF], F32, name="sum_low", tag="sums")
-        result0 = [keep.tile([P, HALF], F32, name=f"result0{h}") for h in range(2)]
         low, high = slice(0, HALF), slice(HALF, U)
-        nc.gpsimd.tensor_tensor(sum_low[:], spread[0][0][:, low], spread[1][0][:, low], ADD)
+        sum_low = keep.tile([P, HALF], F32, name="sum_low")
+        result0 = [keep.tile([P, HALF], F32, name=f"result0_{h}") for h in range(2)]
+        nc.gpsimd.tensor_tensor(sum_low[:], windows[0][0][:, low], windows[1][0][:, low], ADD)
         nc.scalar.activation(result0[0][:], sum_low[:], RELU)
         nc.sync.dma_start(out[0:P, low], result0[0][:])
-        sum_high = spread[0][0][:, low]
-        nc.gpsimd.tensor_tensor(sum_high, spread[0][0][:, high], spread[1][0][:, high], ADD)
+        sum_high = windows[0][0][:, low]
+        quarter = HALF // 2
+        for engine, c0 in ((nc.gpsimd, 0), (nc.vector, quarter)):
+            cols = slice(HALF + c0, HALF + c0 + quarter)
+            engine.tensor_tensor(sum_high[:, c0 : c0 + quarter], windows[0][0][:, cols], windows[1][0][:, cols], ADD)
         nc.scalar.activation(result0[1][:], sum_high, RELU)
         nc.sync.dma_start(out[0:P, high], result0[1][:])
 
-        edges = [0, 192, 384, 512]
-        shares = [slice(a, b) for a, b in zip(edges[:-1], edges[1:])]
-        total = [spread[1][0][:, 0:192], spread[1][0][:, 192:384], spread[1][0][:, edges[2] : U]]
-        result1 = [keep.tile([P, c.stop - c.start], F32, name=f"result1{c.start}") for c in shares]
-
-        for h, cols in enumerate(shares):
-            nc.vector.tensor_tensor(total[h], spread[0][1][:, cols], spread[1][1][:, cols], ADD)
+        shares = [slice(a, b) for a, b in zip(EDGES[:-1], EDGES[1:])]
+        sums1 = windows[1][0]
+        result1 = [keep.tile([P, c.stop - c.start], F32, name=f"result1_{c.start}") for c in shares]
+        for cols in shares:
+            nc.vector.tensor_tensor(sums1[:, cols], windows[0][1][:, cols], windows[1][1][:, cols], ADD)
         for h, cols in enumerate(shares):
             if h == 0:
-                nc.scalar.activation(result1[h][:], total[h], RELU)
+                nc.scalar.activation(result1[h][:], sums1[:, cols], RELU)
             else:
-                nc.vector.tensor_scalar_max(result1[h][:], total[h], 0.0)
+                nc.vector.tensor_scalar_max(result1[h][:], sums1[:, cols], 0.0)
             nc.sync.dma_start(out[P : 2 * P, cols], result1[h][:])

@@ -25,7 +25,8 @@ PIECE = V // 2
 HALF = U // 2
 INNER = (PIECE, V)
 OUTER = (0, V + PIECE)
-EDGES = (0, 192, 384, U)
+EDGES = (0, 128, 384, U)
+REST = 64
 
 
 def tile_picked_spconv_relu_e_kernel(
@@ -62,11 +63,11 @@ def tile_picked_spconv_relu_e_kernel(
         x_planes = xT.rearrange("(p j) t -> j p t", j=PACK)
         for j in range(PACK):
             nc.sync.dma_start(planes[j][:], x_planes[j])
-        nc.sync.dma_start(places[0][:], to1)
+        nc.sync.dma_start(places[1][:], to2)
         load_words(0, w1_words)
         load_words(1, w2_words)
         load_scales(nc.sync, 1, w2_scales, range(1, 4))
-        nc.sync.dma_start(places[1][:], to2)
+        nc.sync.dma_start(places[0][:], to1)
 
         for d, b in ((0, 0), (0, 1), (1, 0)):
             nc.vector.memset(windows[d][b][:], 0.0)
@@ -106,8 +107,7 @@ def tile_picked_spconv_relu_e_kernel(
         for d in (1, 0):
             gather_inner(last, INNER[d], PIECE)
         gather_outer(last)
-        for d in (1, 0):
-            weave(nc.scalar.copy, d, 1)
+        weave(nc.scalar.copy, 1, 1)
 
         def quantise(woven, first):
             cols = slice(first, first + PIECE)
@@ -147,13 +147,15 @@ def tile_picked_spconv_relu_e_kernel(
         for d in (1, 0):
             c0 = (INNER[d] - INNER[0]) * PACK
             quantise(woven_inner[:, c0 : c0 + PIECE * PACK], INNER[d])
-            product(d, 0, INNER[d], tap_banks[d][:, slots[0]])
-            nc.scalar.copy(y_inner0[d][:], tap_banks[d][:, slots[0]])
-        for d in range(2):
-            product(d, 1, INNER[d], inner1_banks[d][:, slots[0]])
-            own_copy[d](y_block1[d][:, in_tap(d, INNER[d])], inner1_banks[d][:, slots[0]])
+        weave(nc.vector.tensor_copy, 0, 1)
         for d in (1, 0):
             quantise(woven_outer[d][:], OUTER[d])
+        for d in (1, 0):
+            product(d, 0, INNER[d], tap_banks[d][:, slots[0]])
+            product(d, 1, INNER[d], inner1_banks[d][:, slots[0]])
+            own_copy[d](y_inner0[d][:], tap_banks[d][:, slots[0]])
+            own_copy[d](y_block1[d][:, in_tap(d, INNER[d])], inner1_banks[d][:, slots[0]])
+        for d in (1, 0):
             for b in range(2):
                 product(d, b, OUTER[d], tap_banks[d][:, slots[1 + b]])
 
@@ -173,22 +175,24 @@ def tile_picked_spconv_relu_e_kernel(
         nc.gpsimd.tensor_tensor(sum_low[:], windows[0][0][:, low], windows[1][0][:, low], ADD)
         nc.scalar.activation(result0[0][:], sum_low[:], RELU)
         nc.sync.dma_start(out[0:P, low], result0[0][:])
-        sum_high = windows[0][0][:, low]
-        quarter = HALF // 2
-        for engine, c0 in ((nc.gpsimd, 0), (nc.vector, quarter)):
-            cols = slice(HALF + c0, HALF + c0 + quarter)
-            engine.tensor_tensor(sum_high[:, c0 : c0 + quarter], windows[0][0][:, cols], windows[1][0][:, cols], ADD)
-        nc.scalar.activation(result0[1][:], sum_high, RELU)
+        sum_high = keep.tile([P, HALF - REST], F32, name="sum_high")
+        parts = ((nc.gpsimd, 0, sum_high[:]), (nc.vector, HALF - REST, windows[0][0][:, 0:REST]))
+        for engine, c0, total in parts:
+            part = slice(c0, c0 + total.shape[1])
+            cols = slice(HALF + part.start, HALF + part.stop)
+            engine.tensor_tensor(total, windows[0][0][:, cols], windows[1][0][:, cols], ADD)
+            nc.scalar.activation(result0[1][:, part], total, RELU)
         nc.sync.dma_start(out[0:P, high], result0[1][:])
 
         shares = [slice(a, b) for a, b in zip(EDGES[:-1], EDGES[1:])]
         sums1 = windows[1][0]
-        result1 = [keep.tile([P, c.stop - c.start], F32, name=f"result1_{c.start}") for c in shares]
+        result1 = keep.tile([P, U], F32, name="result1")
         for cols in shares:
             nc.vector.tensor_tensor(sums1[:, cols], windows[0][1][:, cols], windows[1][1][:, cols], ADD)
-        for h, cols in enumerate(shares):
-            if h == 0:
-                nc.scalar.activation(result1[h][:], sums1[:, cols], RELU)
-            else:
-                nc.vector.tensor_scalar_max(result1[h][:], sums1[:, cols], 0.0)
-            nc.sync.dma_start(out[P : 2 * P, cols], result1[h][:])
+        nc.scalar.activation(result1[:, shares[0]], sums1[:, shares[0]], RELU)
+        nc.sync.dma_start(out[P : 2 * P, shares[0]], result1[:, shares[0]])
+        nc.scalar.activation(result1[:, EDGES[1] : HALF], sums1[:, EDGES[1] : HALF], RELU)
+        nc.vector.tensor_scalar_max(result1[:, HALF : EDGES[2]], sums1[:, HALF : EDGES[2]], 0.0)
+        nc.sync.dma_start(out[P : 2 * P, shares[1]], result1[:, shares[1]])
+        nc.vector.tensor_scalar_max(result1[:, shares[2]], sums1[:, shares[2]], 0.0)
+        nc.sync.dma_start(out[P : 2 * P, shares[2]], result1[:, shares[2]])

from contextlib import ExitStack

import concourse.mybir as mybir

K, T, S, V, N, U = 512, 1024, 512, 256, 256, 512
FLOPS = 2 * K * N * S

F32 = mybir.dt.float32
BF16 = mybir.dt.bfloat16
I32 = mybir.dt.int32
U32 = mybir.dt.uint32
U16 = mybir.dt.uint16
U8 = mybir.dt.uint8
FP8X4 = mybir.dt.float8_e4m3fn_x4
COPY = mybir.ActivationFunctionType.Copy
RELU = mybir.ActivationFunctionType.Relu
ADD = mybir.AluOpType.add

P = 128
PACK = 4
GROUP = 16
QUADRANT = 32
SCALE_ROWS = 4
PIECE = V // 2
HALF = U // 2
INNER = (PIECE, V)
OUTER = (0, V + PIECE)
EDGES = (0, 128, 384, U)
REST = 64


def tile_picked_spconv_relu_e_kernel(
    tc, xT, w1_words, w1_scales, w2_words, w2_scales, offs, to1, to2, out
):
    nc = tc.nc
    with ExitStack() as ctx:
        keep = ctx.enter_context(tc.tile_pool(name="keep", bufs=1))
        psum = ctx.enter_context(tc.psum_pool(name="psum", bufs=1))

        picks = keep.tile([P, S // GROUP], U16, name="picks")
        places = [keep.tile([P, V // GROUP], U16, name=f"places{d}") for d in range(2)]
        planes = [keep.tile([P, T], F32, name=f"plane{j}") for j in range(PACK)]
        w_codes = [keep.tile([P, N], U32, name=f"w_codes{d}", align_bytes=64) for d in range(2)]
        w_scales = keep.tile([P, N], U8, name="w_scales", align_bytes=64)
        windows = [[keep.tile([P, U], F32, name=f"window{d}{b}") for b in range(2)] for d in range(2)]

        nc.gpsimd.memset(w_scales[:].bitcast(I32), 0)

        def load_words(d, words):
            nc.sync.dma_start(w_codes[d][:].bitcast(I32), words[0].rearrange("p n r -> p (n r)").bitcast(I32))

        def load_scales(engine, d, scales, quadrants):
            for q in quadrants:
                first = QUADRANT * q + SCALE_ROWS * d
                engine.dma_start(
                    w_scales[first : first + SCALE_ROWS, :].bitcast(I32),
                    scales[0, SCALE_ROWS * q : SCALE_ROWS * (q + 1), :].bitcast(I32),
                )

        load_scales(nc.scalar, 0, w1_scales, range(4))
        load_scales(nc.scalar, 1, w2_scales, range(1))
        nc.sync.dma_start(picks[:], offs)
        x_planes = xT.rearrange("(p j) t -> j p t", j=PACK)
        for j in range(PACK):
            nc.sync.dma_start(planes[j][:], x_planes[j])
        nc.sync.dma_start(places[1][:], to2)
        load_words(0, w1_words)
        load_words(1, w2_words)
        load_scales(nc.sync, 1, w2_scales, range(1, 4))
        nc.sync.dma_start(places[0][:], to1)

        for d, b in ((0, 0), (0, 1), (1, 0)):
            nc.vector.memset(windows[d][b][:], 0.0)
        nc.scalar.activation(windows[1][1][:], windows[0][0][:], COPY)

        x_codes = keep.tile([P, S], U32, name="x_codes", align_bytes=64)
        x_scales = keep.tile([P, S], U8, name="x_scales", align_bytes=64)
        woven_inner = keep.tile([P, 2 * PIECE * PACK], BF16, name="woven_inner", align_bytes=64)
        woven_outer = [keep.tile([P, PIECE * PACK], BF16, name=f"woven_outer{d}", align_bytes=64) for d in range(2)]
        staged = [keep.tile([P, PACK, PIECE], BF16, name=f"staged{d}") for d in range(2)]

        def by_voxel(woven):
            return woven[:].rearrange("p (c j) -> p c j", j=PACK)

        def picked(j, first, count):
            return planes[j][:].indirect(picks[:, first // GROUP : (first + count) // GROUP])

        def gather_inner(j, first, count):
            c0 = first - INNER[0]
            nc.vector.tensor_copy(by_voxel(woven_inner)[:, c0 : c0 + count, j], picked(j, first, count))

        def gather_outer(j):
            for d in (1, 0):
                nc.scalar.activation(staged[d][:, j, :], picked(j, OUTER[d], PIECE), COPY)

        def weave(copy, d, pair):
            js = slice(2 * pair, 2 * pair + 2)
            copy(by_voxel(woven_outer[d])[:, :, js], staged[d][:, js, :].rearrange("p j c -> p c j"))

        last = PACK - 1
        for j in range(last):
            gather_inner(j, INNER[0], 2 * PIECE)
            gather_outer(j)
            if j == 1:
                weave(nc.vector.tensor_copy, 1, 0)
                weave(nc.scalar.copy, 0, 0)
        for d in (1, 0):
            gather_inner(last, INNER[d], PIECE)
        gather_outer(last)
        weave(nc.scalar.copy, 1, 1)

        def quantise(woven, first):
            cols = slice(first, first + PIECE)
            nc.vector.quantize_mx(out=x_codes[:, cols].bitcast(FP8X4), scales=x_scales[:, cols], in_=woven)

        def product(d, b, first, acc):
            m_cols = slice(b * P, (b + 1) * P)
            cols = slice(first, first + PIECE)
            nc.tensor.matmul_mx(
                out=acc,
                lhsT=w_codes[d][:, m_cols].bitcast(FP8X4),
                lhsT_scale=w_scales[SCALE_ROWS * d : P, m_cols],
                rhs=x_codes[:, cols].bitcast(FP8X4),
                rhs_scale=x_scales[:, cols],
                start=True,
                stop=True,
            )

        def scatter(d, b, first, count, y):
            target = windows[d][b][:].indirect(places[d][:, first // GROUP : (first + count) // GROUP])
            if d == 0:
                nc.vector.tensor_copy(target, y)
            else:
                nc.scalar.activation(target, y, COPY)

        tap_banks = [psum.tile([P, U], F32, name=f"tap_bank{d}") for d in range(2)]
        inner1_banks = [psum.tile([P, U], F32, name=f"inner1_bank{d}") for d in range(2)]
        slots = [slice(i * PIECE, (i + 1) * PIECE) for i in range(3)]
        own_copy = (nc.vector.tensor_copy, nc.scalar.copy)
        y_outer0 = [keep.tile([P, PIECE], F32, name=f"y_outer0_{d}") for d in range(2)]
        y_block1 = [keep.tile([P, V], F32, name=f"y_block1_{d}") for d in range(2)]
        y_inner0 = [keep.tile([P, PIECE], F32, name=f"y_inner0_{d}") for d in range(2)]

        def in_tap(d, first):
            return slice(first - d * V, first - d * V + PIECE)

        for d in (1, 0):
            c0 = (INNER[d] - INNER[0]) * PACK
            quantise(woven_inner[:, c0 : c0 + PIECE * PACK], INNER[d])
        weave(nc.vector.tensor_copy, 0, 1)
        for d in (1, 0):
            quantise(woven_outer[d][:], OUTER[d])
        for d in (1, 0):
            product(d, 0, INNER[d], tap_banks[d][:, slots[0]])
            product(d, 1, INNER[d], inner1_banks[d][:, slots[0]])
            own_copy[d](y_inner0[d][:], tap_banks[d][:, slots[0]])
            own_copy[d](y_block1[d][:, in_tap(d, INNER[d])], inner1_banks[d][:, slots[0]])
        for d in (1, 0):
            for b in range(2):
                product(d, b, OUTER[d], tap_banks[d][:, slots[1 + b]])

        for d in range(2):
            scatter(d, 0, INNER[d] - d * V, PIECE, y_inner0[d][:])
        for d in (1, 0):
            own_copy[d](y_outer0[d][:], tap_banks[d][:, slots[1]])
            own_copy[d](y_block1[d][:, in_tap(d, OUTER[d])], tap_banks[d][:, slots[2]])
        for d in range(2):
            scatter(d, 0, OUTER[d] - d * V, PIECE, y_outer0[d][:])
        for d in range(2):
            scatter(d, 1, 0, V, y_block1[d][:])

        low, high = slice(0, HALF), slice(HALF, U)
        sum_low = keep.tile([P, HALF], F32, name="sum_low")
        result0 = [keep.tile([P, HALF], F32, name=f"result0_{h}") for h in range(2)]
        nc.gpsimd.tensor_tensor(sum_low[:], windows[0][0][:, low], windows[1][0][:, low], ADD)
        nc.scalar.activation(result0[0][:], sum_low[:], RELU)
        nc.sync.dma_start(out[0:P, low], result0[0][:])
        sum_high = keep.tile([P, HALF - REST], F32, name="sum_high")
        parts = ((nc.gpsimd, 0, sum_high[:]), (nc.vector, HALF - REST, windows[0][0][:, 0:REST]))
        for engine, c0, total in parts:
            part = slice(c0, c0 + total.shape[1])
            cols = slice(HALF + part.start, HALF + part.stop)
            engine.tensor_tensor(total, windows[0][0][:, cols], windows[1][0][:, cols], ADD)
            nc.scalar.activation(result0[1][:, part], total, RELU)
        nc.sync.dma_start(out[0:P, high], result0[1][:])

        shares = [slice(a, b) for a, b in zip(EDGES[:-1], EDGES[1:])]
        sums1 = windows[1][0]
        result1 = keep.tile([P, U], F32, name="result1")
        for cols in shares:
            nc.vector.tensor_tensor(sums1[:, cols], windows[0][1][:, cols], windows[1][1][:, cols], ADD)
        nc.scalar.activation(result1[:, shares[0]], sums1[:, shares[0]], RELU)
        nc.sync.dma_start(out[P : 2 * P, shares[0]], result1[:, shares[0]])
        nc.scalar.activation(result1[:, EDGES[1] : HALF], sums1[:, EDGES[1] : HALF], RELU)
        nc.vector.tensor_scalar_max(result1[:, HALF : EDGES[2]], sums1[:, HALF : EDGES[2]], 0.0)
        nc.sync.dma_start(out[P : 2 * P, shares[1]], result1[:, shares[1]])
        nc.vector.tensor_scalar_max(result1[:, shares[2]], sums1[:, shares[2]], 0.0)
        nc.sync.dma_start(out[P : 2 * P, shares[2]], result1[:, shares[2]])
